import numpy as np
import ml_dtypes


def mxq(x, axis, fmt="e4m3"):
    dtype, down = {"e4m3": (ml_dtypes.float8_e4m3fn, 7), "e5m2": (ml_dtypes.float8_e5m2, 14)}[fmt]
    v = np.moveaxis(np.asarray(x, np.float32).astype(ml_dtypes.bfloat16).astype(np.float64), axis, -1)
    blocks = v.reshape(v.shape[:-1] + (-1, 32))
    amax = np.abs(blocks).max(-1, keepdims=True)
    byte = np.maximum(np.where(amax > 0, np.frexp(amax)[1] - 1 + 127, 0) - down, 1)
    scale = np.exp2(byte - 127.0)
    codes = (blocks / scale).astype(np.float32).astype(dtype).astype(np.float64)
    return np.moveaxis((codes * scale).reshape(v.shape), -1, axis)


WIDE = False


def mx_kscale(k):
    if not WIDE:
        return np.ones(k)
    levels = np.array([10, -10, 5, -5, 0])
    if k % 512:
        return np.exp2(np.random.permutation(np.resize(levels, k // 32))).repeat(32)
    a = np.empty((k // 512, 16))
    for p in range(k // 512):
        a[p, :8] = np.random.permutation(np.resize(levels, 8))
        for g in range(8):
            far = levels[np.abs(levels - a[p, g]) >= 10]
            a[p, g + 8] = far[np.random.randint(len(far))]
    return np.exp2(a.ravel()).repeat(32)


def f64(x):
    return np.asarray(x).astype(np.float64)


def striped(idx):
    return np.tile(idx.reshape(-1, 16).T, (8, 1)).astype(np.uint16)


def unstriped(offs):
    return offs[:16].T.reshape(-1).astype(np.int64)


E2M1 = np.array([0.0, 0.5, 1.0, 1.5, 2.0, 3.0, 4.0, 6.0, -0.0, -0.5, -1.0, -1.5, -2.0, -3.0, -4.0, -6.0])


def pack_weight(w, fmt):
    k, n = w.shape
    w = f64(np.asarray(w, np.float32).astype(ml_dtypes.bfloat16)).reshape(k // 32, 32, n)
    amax = np.abs(w).max(1)
    if fmt == "e4m3":
        byte = np.frexp(amax)[1] - 1 + 127 - 7
    else:
        mant, ex = np.frexp(amax / 6.0)
        byte = np.where(mant > 0.5, ex, ex - 1) + 127
    byte = np.clip(np.where(amax > 0, byte, 1), 1, 254)
    scaled = (w * np.exp2(127.0 - byte)[:, None, :]).reshape(k, n).astype(np.float32)
    by_word = np.ascontiguousarray(scaled.reshape(k // 512, 128, 4, n).transpose(0, 1, 3, 2))
    if fmt == "e4m3":
        words = by_word.astype(ml_dtypes.float8_e4m3fn).view(np.uint8)
    else:
        c = by_word.astype(ml_dtypes.float4_e2m1fn).view(np.uint8) & 0xF
        words = (c[..., 0::2] | (c[..., 1::2] << 4)).reshape(k // 512, 128, 2 * n)
    return np.ascontiguousarray(words), np.ascontiguousarray(byte.astype(np.uint8).reshape(k // 512, 16, n))


def unpack_weight(words, scales, fmt):
    g, _, n = scales.shape
    words = np.ascontiguousarray(words).reshape(g, 128, n, -1)
    if fmt == "e4m3":
        vals = words.view(ml_dtypes.float8_e4m3fn).astype(np.float64)
    else:
        nib = np.empty((g, 128, n, 4), np.uint8)
        nib[..., 0::2] = words & 0xF
        nib[..., 1::2] = words >> 4
        vals = E2M1[nib]
    vals = vals * np.repeat(np.exp2(scales.astype(np.float64) - 127.0), 8, axis=1)[..., None]
    return vals.transpose(0, 1, 3, 2).reshape(g * 512, n)


def gelu(v):
    return 0.5 * v * (1.0 + np.tanh(np.sqrt(2.0 / np.pi) * (v + 0.044715 * v**3)))


def striped8(idx):
    return np.concatenate([v.reshape(-1, 16).T for v in idx]).astype(np.uint16)


def unstriped8(offs):
    return np.stack([offs[16 * g:16 * g + 16].T.reshape(-1) for g in range(8)]).astype(np.int64)


def heads(xT, wgt, idx8):
    k = np.arange(xT.shape[0])
    return wgt[k // 4 % 128] * xT[k[:, None], idx8[k % 512 // 64]]


K, T, S, H, G, R = 1024, 2048, 1024, 512, 8, 16

def setup_inputs():
    n = np.random.standard_normal
    s = mx_kscale(K)[:, None]
    u = mx_kscale(H)[:, None]
    w2_words, w2_scales = pack_weight(1.5 * n((H, K)) / np.sqrt(H) / u * s.T, "e2m1")
    lists = np.stack([np.random.permutation(T)[:S] for _ in range(G)])
    return {
        "xT": (n((K, T)) * s).astype(np.float32),
        "wgt": np.repeat(np.random.uniform(0.5, 2.0, (G, S)), R, axis=0).astype(np.float32),
        "offs": striped8(lists),
        "w1": (n((K, H)) / np.sqrt(K) / s).astype(np.float32),
        "gain": (np.random.uniform(0.5, 1.5, H) * u[:, 0]).astype(np.float32),
        "w2_words": w2_words,
        "w2_scales": w2_scales,
        "prec": (np.random.uniform(0.4, 1.0, K) / s[:, 0]).astype(np.float32),
    }

def reference(xT, wgt, offs, w1, gain, w2_words, w2_scales, prec):
    xg = heads(f64(xT), f64(wgt), unstriped8(offs))
    xq = mxq(xg, 0, "e4m3")
    w1q = mxq(f64(w1), 0, "e4m3")
    h = np.tanh(w1q.T @ xq) * f64(gain)[:, None]
    hq = mxq(h, 0, "e4m3")
    w2 = unpack_weight(w2_words, w2_scales, "e2m1")
    rec = w2.T @ hq
    return np.square((rec - xg) * f64(prec)[:, None])

@@ -1,0 +1,209 @@
+from contextlib import ExitStack
+
+import concourse.mybir as mybir
+
+K, T, S, H = 1024, 2048, 1024, 512
+FLOPS = 2 * 2 * K * H * S
+
+F32 = mybir.dt.float32
+BF16 = mybir.dt.bfloat16
+I32 = mybir.dt.int32
+U32 = mybir.dt.uint32
+U16 = mybir.dt.uint16
+U8 = mybir.dt.uint8
+E4M3X4 = mybir.dt.float8_e4m3fn_x4
+E2M1X4 = mybir.dt.float4_e2m1fn_x4
+ACT = mybir.ActivationFunctionType
+ALU = mybir.AluOpType
+
+P = 128
+PACK = 4
+PASSES = 2
+HALF = 512
+QUARTER = 256
+N1 = 128
+LINE = 4
+
+
+def tile_list_camera_error_maps_kernel(tc, xT, wgt, offs, w1, gain, w2_words, w2_scales, prec, out):
+    nc = tc.nc
+    x_planes = xT.rearrange("(a p i) t -> a i p t", a=PASSES, i=PACK)
+    out_planes = out.rearrange("(a p i) j -> a i p j", a=PASSES, i=PACK)
+    w1_rows = w1.rearrange("(a p i) r -> a p i r", a=PASSES, i=PACK)
+
+    with ExitStack() as ctx:
+        keep = ctx.enter_context(tc.tile_pool(name="keep", bufs=1))
+        ring = ctx.enter_context(tc.tile_pool(name="ring", bufs=4))
+        hps = ctx.enter_context(tc.psum_pool(name="hps", bufs=3))
+        rps = ctx.enter_context(tc.psum_pool(name="rps", bufs=5))
+
+        offsets = keep.tile([P, S // 16], U16, name="offsets")
+        w2_raw = keep.tile([P, 2 * K], U8, name="w2_raw", align_bytes=64)
+        s2_raw = keep.tile([P, K], U8, name="s2_raw", align_bytes=64)
+        w2_codes = keep.tile([P, 2 * K], U8, name="w2_codes", align_bytes=64)
+        w2_plane = keep.tile([P, K], U8, name="w2_plane", align_bytes=64)
+        wgt_sb = [keep.tile([P, HALF], F32, name="wgt0", tag="late"), keep.tile([P, HALF], F32, name="wgt1")]
+        x_sb = [[keep.tile([P, T], F32, name="x%d%d" % (a, i)) for i in range(PACK)] for a in range(PASSES)]
+        w1_raw = [keep.tile([P, PACK, H], F32, name="w1raw%d" % a) for a in range(PASSES)]
+        gain_sb = keep.tile([P, PACK], F32, name="gain_sb")
+        prec_sb = keep.tile([P, PASSES, PACK], F32, name="prec_sb")
+        warm = keep.tile([P, 1], F32, name="warm")
+
+        xg = [[keep.tile([P, PACK, HALF], F32, name="xg%d%d" % (a, h), tag=("late" if a + h == 2 else "xg%d%d" % (a, h))) for h in range(2)] for a in range(PASSES)]
+        xb = [[keep.tile([P, HALF * PACK], BF16, name="xb%d%d" % (a, h), align_bytes=64) for h in range(2)] for a in range(PASSES)]
+        x_codes = [[keep.tile([P, HALF], U32, name="xc%d%d" % (a, h), align_bytes=64) for h in range(2)] for a in range(PASSES)]
+        x_plane = [[keep.tile([P, HALF], U8, name="xs%d%d" % (a, h), align_bytes=64) for h in range(2)] for a in range(PASSES)]
+        w1b = [keep.tile([P, H * PACK], BF16, name="w1b%d" % a, align_bytes=64) for a in range(PASSES)]
+        w1_codes = [keep.tile([P, H], U32, name="w1c%d" % a, align_bytes=64) for a in range(PASSES)]
+        w1_plane = [keep.tile([P, H], U8, name="w1s%d" % a, align_bytes=64) for a in range(PASSES)]
+        th = [keep.tile([P, QUARTER * PACK], F32, name="th%d" % c) for c in range(4)]
+        hb = [keep.tile([P, HALF * PACK], BF16, name="hb%d" % h, align_bytes=64) for h in range(2)]
+        h_codes = [keep.tile([P, HALF], U32, name="hc%d" % h, align_bytes=64) for h in range(2)]
+        h_plane = [keep.tile([P, HALF], U8, name="hs%d" % h, align_bytes=64) for h in range(2)]
+
+        nc.vector.memset(s2_raw[:].bitcast(U32), 0)
+        nc.vector.memset(warm[:], 0.0)
+        nc.sync.dma_start(offsets[:], offs)
+        nc.sync.dma_start(w2_raw[:].bitcast(I32), w2_words[0].bitcast(I32))
+        nc.sync.dma_start(wgt_sb[0][:], wgt[:, 0:HALF])
+        nc.sync.dma_start(x_sb[0][0][:], x_planes[0, 0])
+        scale_rows = w2_scales[0].bitcast(I32)
+        for q in range(4):
+            nc.scalar.dma_start(s2_raw[32 * q : 32 * q + 4, :].bitcast(I32), scale_rows[4 * q : 4 * q + 4, :])
+        nc.scalar.activation(warm[:], warm[:], ACT.Tanh)
+        nc.sync.dma_start(wgt_sb[1][:], wgt[:, HALF:S])
+        for i in range(1, PACK):
+            nc.sync.dma_start(x_sb[0][i][:], x_planes[0, i])
+        nc.sync.dma_start(gain_sb[:], gain.rearrange("(p t) -> p t", t=PACK))
+        nc.sync.dma_start(prec_sb[:], prec.rearrange("(a p i) -> p a i", a=PASSES, i=PACK))
+        nc.sync.dma_start(w1_raw[0][:], w1_rows[0])
+        nc.sync.dma_start(w1_raw[1][:], w1_rows[1])
+        for i in range(PACK):
+            nc.sync.dma_start(x_sb[1][i][:], x_planes[1, i])
+
+        nc.vector.tensor_copy(
+            w2_codes[:].rearrange("p (a i q b) -> p a i q b", a=PASSES, i=PACK, b=2),
+            w2_raw[:].rearrange("p (a q i b) -> p a i q b", a=PASSES, i=PACK, b=2),
+        )
+        nc.vector.tensor_copy(
+            w2_plane[:].rearrange("p (a i q) -> p a i q", a=PASSES, i=PACK),
+            s2_raw[:].rearrange("p (a q i) -> p a i q", a=PASSES, i=PACK),
+        )
+
+        def gather(a, i, h):
+            window = x_sb[a][i][:].indirect(offsets[:, h * HALF // 16 : (h + 1) * HALF // 16])
+            nc.vector.tensor_tensor(xg[a][h][:, i, :], window, wgt_sb[h][:], ALU.mult)
+
+        def weave_x(a, h, c0, n):
+            nc.scalar.copy(
+                xb[a][h][:, c0 * PACK : (c0 + n) * PACK].rearrange("p (c e i) -> p c i e", e=LINE, i=PACK),
+                xg[a][h][:, :, c0 : c0 + n].rearrange("p i (c e) -> p c i e", e=LINE),
+            )
+
+        def quant_x(a, h, c0, n):
+            nc.vector.quantize_mx(
+                x_codes[a][h][:, c0 : c0 + n].bitcast(E4M3X4),
+                x_plane[a][h][:, c0 : c0 + n],
+                xb[a][h][:, c0 * PACK : (c0 + n) * PACK],
+            )
+
+        def w1_views(a):
+            return (
+                w1b[a][:].rearrange("p (t m i) -> p m i t", t=PACK, i=PACK),
+                w1_raw[a][:].rearrange("p i (m t) -> p m i t", t=PACK),
+            )
+
+        def quant_w1(a):
+            nc.vector.quantize_mx(w1_codes[a][:].bitcast(E4M3X4), w1_plane[a][:], w1b[a][:])
+
+        def encode(c):
+            h = c // 2
+            for u in range(2):
+                n0 = (c % 2) * QUARTER + u * N1
+                bank = hps.tile([P, PACK, N1], F32, name="hbank")
+                for t in range(PACK):
+                    for a in range(PASSES):
+                        nc.tensor.matmul_mx(
+                            bank[:, t, :],
+                            lhsT=w1_codes[a][:, t * P : (t + 1) * P].bitcast(E4M3X4),
+                            lhsT_scale=w1_plane[a][:, t * P : (t + 1) * P],
+                            rhs=x_codes[a][h][:, n0 : n0 + N1].bitcast(E4M3X4),
+                            rhs_scale=x_plane[a][h][:, n0 : n0 + N1],
+                            start=(a == 0),
+                            stop=(a == PASSES - 1),
+                        )
+                nc.scalar.activation(
+                    th[c][:, u * N1 * PACK : (u + 1) * N1 * PACK].rearrange("p (n t) -> p n t", t=PACK),
+                    bank[:].rearrange("p t n -> p n t"),
+                    ACT.Tanh,
+                )
+
+        def apply_gain(c):
+            h = c // 2
+            c0 = (c % 2) * QUARTER * PACK
+            nc.vector.tensor_tensor(
+                hb[h][:, c0 : c0 + QUARTER * PACK].rearrange("p (n t) -> p n t", t=PACK),
+                th[c][:].rearrange("p (n t) -> p n t", t=PACK),
+                gain_sb[:].unsqueeze(1).to_broadcast([P, QUARTER, PACK]),
+                ALU.mult,
+            )
+
+        def quant_h(h):
+            nc.vector.quantize_mx(h_codes[h][:].bitcast(E4M3X4), h_plane[h][:], hb[h][:])
+
+        def decode(h, a, i):
+            g = a * PACK + i
+            bank = rps.tile([P, HALF], F32, name="rbank")
+            nc.tensor.matmul_mx(
+                bank[:],
+                lhsT=w2_codes[:, g * 2 * P : (g + 1) * 2 * P].bitcast(E2M1X4),
+                lhsT_scale=w2_plane[:, g * P : (g + 1) * P],
+                rhs=h_codes[h][:].bitcast(E4M3X4),
+                rhs_scale=h_plane[h][:],
+                start=True,
+                stop=True,
+            )
+            diff = ring.tile([P, HALF], F32, name="diff")
+            nc.vector.tensor_tensor(diff[:], bank[:], xg[a][h][:, i, :], ALU.subtract)
+            err = ring.tile([P, HALF], F32, name="err", bufs=8)
+            nc.scalar.activation(err[:], diff[:], ACT.Square, scale=prec_sb[:, a, i : i + 1])
+            nc.sync.dma_start(out_planes[a, i][:, h * HALF : (h + 1) * HALF], err[:])
+
+        for i in range(PACK):
+            for h in range(2):
+                gather(0, i, h)
+        for a in range(PASSES):
+            nc.scalar.copy(*w1_views(a))
+            weave_x(0, a, 0, HALF)
+        for a in range(PASSES):
+            quant_w1(a)
+            quant_x(0, a, 0, HALF)
+        for i in range(PACK):
+            gather(1, i, 0)
+        for c in range(2):
+            weave_x(1, 0, c * QUARTER, QUARTER)
+            quant_x(1, 0, c * QUARTER, QUARTER)
+        for i in range(PACK):
+            gather(1, i, 1)
+        encode(0)
+        encode(1)
+        for c in range(2):
+            weave_x(1, 1, c * QUARTER, QUARTER)
+        apply_gain(0)
+        apply_gain(1)
+        quant_x(1, 1, 0, QUARTER)
+        quant_h(0)
+        quant_x(1, 1, QUARTER, QUARTER)
+        encode(2)
+        for g in range(4):
+            decode(0, 0, g)
+        encode(3)
+        apply_gain(2)
+        decode(0, 1, 0)
+        apply_gain(3)
+        decode(0, 1, 1)
+        quant_h(1)
+        decode(0, 1, 2)
+        decode(0, 1, 3)
+        for g in range(PASSES * PACK):
+            decode(1, g // PACK, g % PACK)

@@ -34,52 +34,53 @@ def tile_list_camera_error_maps_kernel(tc, xT, wgt, offs, w1, gain, w2_words, w2
     with ExitStack() as ctx:
         keep = ctx.enter_context(tc.tile_pool(name="keep", bufs=1))
         ring = ctx.enter_context(tc.tile_pool(name="ring", bufs=4))
-        hps = ctx.enter_context(tc.psum_pool(name="hps", bufs=3))
-        rps = ctx.enter_context(tc.psum_pool(name="rps", bufs=5))
+        psum = ctx.enter_context(tc.psum_pool(name="psum", bufs=8))
 
         offsets = keep.tile([P, S // 16], U16, name="offsets")
         w2_raw = keep.tile([P, 2 * K], U8, name="w2_raw", align_bytes=64)
         s2_raw = keep.tile([P, K], U8, name="s2_raw", align_bytes=64)
         w2_codes = keep.tile([P, 2 * K], U8, name="w2_codes", align_bytes=64)
         w2_plane = keep.tile([P, K], U8, name="w2_plane", align_bytes=64)
-        wgt_sb = [keep.tile([P, HALF], F32, name="wgt0", tag="late"), keep.tile([P, HALF], F32, name="wgt1")]
-        x_sb = [[keep.tile([P, T], F32, name="x%d%d" % (a, i)) for i in range(PACK)] for a in range(PASSES)]
+        wgt_sb = keep.tile([P, S], F32, name="wgt_sb")
+        x_sb = [[keep.tile([P, T], F32, name="x%d%d" % (a, i), align_bytes=64) for i in range(PACK)] for a in range(PASSES)]
         w1_raw = [keep.tile([P, PACK, H], F32, name="w1raw%d" % a) for a in range(PASSES)]
         gain_sb = keep.tile([P, PACK], F32, name="gain_sb")
         prec_sb = keep.tile([P, PASSES, PACK], F32, name="prec_sb")
         warm = keep.tile([P, 1], F32, name="warm")
 
-        xg = [[keep.tile([P, PACK, HALF], F32, name="xg%d%d" % (a, h), tag=("late" if a + h == 2 else "xg%d%d" % (a, h))) for h in range(2)] for a in range(PASSES)]
-        xb = [[keep.tile([P, HALF * PACK], BF16, name="xb%d%d" % (a, h), align_bytes=64) for h in range(2)] for a in range(PASSES)]
-        x_codes = [[keep.tile([P, HALF], U32, name="xc%d%d" % (a, h), align_bytes=64) for h in range(2)] for a in range(PASSES)]
-        x_plane = [[keep.tile([P, HALF], U8, name="xs%d%d" % (a, h), align_bytes=64) for h in range(2)] for a in range(PASSES)]
+        xg = [keep.tile([P, PACK, S], F32, name="xg%d" % a) for a in range(PASSES)]
+        xb = [keep.tile([P, S * PACK], BF16, name="xb%d" % a, align_bytes=64) for a in range(PASSES)]
+        after_x11 = keep.tile([P, S + H], U32, name="after_x11", tag="x11", align_bytes=64)
+        x_codes = [after_x11[:, 0:S], keep.tile([P, S], U32, name="xc1", align_bytes=64)]
+        x_plane = [keep.tile([P, S], U8, name="xs%d" % a, align_bytes=64) for a in range(PASSES)]
         w1b = [keep.tile([P, H * PACK], BF16, name="w1b%d" % a, align_bytes=64) for a in range(PASSES)]
-        w1_codes = [keep.tile([P, H], U32, name="w1c%d" % a, align_bytes=64) for a in range(PASSES)]
+        w1_codes = [keep.tile([P, H], U32, name="w1c0", align_bytes=64), after_x11[:, S : S + H]]
         w1_plane = [keep.tile([P, H], U8, name="w1s%d" % a, align_bytes=64) for a in range(PASSES)]
-        th = [keep.tile([P, QUARTER * PACK], F32, name="th%d" % c) for c in range(4)]
+        th = keep.tile([P, S * PACK], F32, name="th")
         hb = [keep.tile([P, HALF * PACK], BF16, name="hb%d" % h, align_bytes=64) for h in range(2)]
         h_codes = [keep.tile([P, HALF], U32, name="hc%d" % h, align_bytes=64) for h in range(2)]
         h_plane = [keep.tile([P, HALF], U8, name="hs%d" % h, align_bytes=64) for h in range(2)]
 
-        nc.vector.memset(s2_raw[:].bitcast(U32), 0)
-        nc.vector.memset(warm[:], 0.0)
+        nc.gpsimd.memset(s2_raw[:].bitcast(U32), 0)
+        nc.gpsimd.memset(warm[:], 0.0)
         nc.sync.dma_start(offsets[:], offs)
         nc.sync.dma_start(w2_raw[:].bitcast(I32), w2_words[0].bitcast(I32))
-        nc.sync.dma_start(wgt_sb[0][:], wgt[:, 0:HALF])
+        nc.sync.dma_start(wgt_sb[:, 0:HALF], wgt[:, 0:HALF])
         nc.sync.dma_start(x_sb[0][0][:], x_planes[0, 0])
         scale_rows = w2_scales[0].bitcast(I32)
         for q in range(4):
-            nc.scalar.dma_start(s2_raw[32 * q : 32 * q + 4, :].bitcast(I32), scale_rows[4 * q : 4 * q + 4, :])
+            nc.sync.dma_start(s2_raw[32 * q : 32 * q + 4, :].bitcast(I32), scale_rows[4 * q : 4 * q + 4, :])
         nc.scalar.activation(warm[:], warm[:], ACT.Tanh)
-        nc.sync.dma_start(wgt_sb[1][:], wgt[:, HALF:S])
+        nc.sync.dma_start(wgt_sb[:, HALF:S], wgt[:, HALF:S])
         for i in range(1, PACK):
             nc.sync.dma_start(x_sb[0][i][:], x_planes[0, i])
         nc.sync.dma_start(gain_sb[:], gain.rearrange("(p t) -> p t", t=PACK))
         nc.sync.dma_start(prec_sb[:], prec.rearrange("(a p i) -> p a i", a=PASSES, i=PACK))
-        nc.sync.dma_start(w1_raw[0][:], w1_rows[0])
-        nc.sync.dma_start(w1_raw[1][:], w1_rows[1])
-        for i in range(PACK):
+        for i in range(2):
             nc.sync.dma_start(x_sb[1][i][:], x_planes[1, i])
+        for i in range(2):
+            nc.sync.dma_start(w1_raw[1 - i][:], w1_rows[1 - i])
+            nc.sync.dma_start(x_sb[1][2 + i][:], x_planes[1, 2 + i])
 
         nc.vector.tensor_copy(
             w2_codes[:].rearrange("p (a i q b) -> p a i q b", a=PASSES, i=PACK, b=2),
@@ -90,21 +91,21 @@ def tile_list_camera_error_maps_kernel(tc, xT, wgt, offs, w1, gain, w2_words, w2
             s2_raw[:].rearrange("p (a q i) -> p a i q", a=PASSES, i=PACK),
         )
 
-        def gather(a, i, h):
-            window = x_sb[a][i][:].indirect(offsets[:, h * HALF // 16 : (h + 1) * HALF // 16])
-            nc.vector.tensor_tensor(xg[a][h][:, i, :], window, wgt_sb[h][:], ALU.mult)
+        def gather(a, i, c0, n):
+            window = x_sb[a][i][:].indirect(offsets[:, c0 // 16 : (c0 + n) // 16])
+            nc.vector.tensor_tensor(xg[a][:, i, c0 : c0 + n], window, wgt_sb[:, c0 : c0 + n], ALU.mult)
 
-        def weave_x(a, h, c0, n):
-            nc.scalar.copy(
-                xb[a][h][:, c0 * PACK : (c0 + n) * PACK].rearrange("p (c e i) -> p c i e", e=LINE, i=PACK),
-                xg[a][h][:, :, c0 : c0 + n].rearrange("p i (c e) -> p c i e", e=LINE),
+        def weave_x(a, c0, n, copy):
+            copy(
+                xb[a][:, c0 * PACK : (c0 + n) * PACK].rearrange("p (c e i) -> p c i e", e=LINE, i=PACK),
+                xg[a][:, :, c0 : c0 + n].rearrange("p i (c e) -> p c i e", e=LINE),
             )
 
-        def quant_x(a, h, c0, n):
+        def quant_x(a, c0, n):
             nc.vector.quantize_mx(
-                x_codes[a][h][:, c0 : c0 + n].bitcast(E4M3X4),
-                x_plane[a][h][:, c0 : c0 + n],
-                xb[a][h][:, c0 * PACK : (c0 + n) * PACK],
+                x_codes[a][:, c0 : c0 + n].bitcast(E4M3X4),
+                x_plane[a][:, c0 : c0 + n],
+                xb[a][:, c0 * PACK : (c0 + n) * PACK],
             )
 
         def w1_views(a):
@@ -114,46 +115,48 @@ def tile_list_camera_error_maps_kernel(tc, xT, wgt, offs, w1, gain, w2_words, w2
             )
 
         def quant_w1(a):
-            nc.vector.quantize_mx(w1_codes[a][:].bitcast(E4M3X4), w1_plane[a][:], w1b[a][:])
+            nc.vector.quantize_mx(w1_codes[a][:, 0:H].bitcast(E4M3X4), w1_plane[a][:], w1b[a][:])
 
-        def encode(c):
-            h = c // 2
-            for u in range(2):
-                n0 = (c % 2) * QUARTER + u * N1
-                bank = hps.tile([P, PACK, N1], F32, name="hbank")
-                for t in range(PACK):
-                    for a in range(PASSES):
-                        nc.tensor.matmul_mx(
-                            bank[:, t, :],
-                            lhsT=w1_codes[a][:, t * P : (t + 1) * P].bitcast(E4M3X4),
-                            lhsT_scale=w1_plane[a][:, t * P : (t + 1) * P],
-                            rhs=x_codes[a][h][:, n0 : n0 + N1].bitcast(E4M3X4),
-                            rhs_scale=x_plane[a][h][:, n0 : n0 + N1],
-                            start=(a == 0),
-                            stop=(a == PASSES - 1),
-                        )
-                nc.scalar.activation(
-                    th[c][:, u * N1 * PACK : (u + 1) * N1 * PACK].rearrange("p (n t) -> p n t", t=PACK),
-                    bank[:].rearrange("p t n -> p n t"),
-                    ACT.Tanh,
-                )
+        banks = [psum.tile([P, PACK, N1], F32, name="hbank%d" % b, tag="bank") for b in range(S // N1)]
 
-        def apply_gain(c):
-            h = c // 2
-            c0 = (c % 2) * QUARTER * PACK
+        def encode_pass(b, t, a):
+            nc.tensor.matmul_mx(
+                banks[b][:, t, :],
+                lhsT=w1_codes[a][:, t * P : (t + 1) * P].bitcast(E4M3X4),
+                lhsT_scale=w1_plane[a][:, t * P : (t + 1) * P],
+                rhs=x_codes[a][:, b * N1 : (b + 1) * N1].bitcast(E4M3X4),
+                rhs_scale=x_plane[a][:, b * N1 : (b + 1) * N1],
+                start=(a == 0),
+                stop=(a == PASSES - 1),
+            )
+
+        def encode(b):
+            for t in range(PACK):
+                for a in range(PASSES):
+                    if (t, a) != (0, 0):
+                        encode_pass(b, t, a)
+            nc.scalar.activation(
+                th[:, b * N1 * PACK : (b + 1) * N1 * PACK].rearrange("p (n t) -> p n t", t=PACK),
+                banks[b][:].rearrange("p t n -> p n t"),
+                ACT.Tanh,
+            )
+
+        def apply_gain(c0, n):
+            h = c0 // HALF
+            o = (c0 - h * HALF) * PACK
             nc.vector.tensor_tensor(
-                hb[h][:, c0 : c0 + QUARTER * PACK].rearrange("p (n t) -> p n t", t=PACK),
-                th[c][:].rearrange("p (n t) -> p n t", t=PACK),
-                gain_sb[:].unsqueeze(1).to_broadcast([P, QUARTER, PACK]),
+                hb[h][:, o : o + n * PACK].rearrange("p (n t) -> p n t", t=PACK),
+                th[:, c0 * PACK : (c0 + n) * PACK].rearrange("p (n t) -> p n t", t=PACK),
+                gain_sb[:].unsqueeze(1).to_broadcast([P, n, PACK]),
                 ALU.mult,
             )
 
         def quant_h(h):
             nc.vector.quantize_mx(h_codes[h][:].bitcast(E4M3X4), h_plane[h][:], hb[h][:])
 
-        def decode(h, a, i):
+        def decode(h, a, i, step=HALF):
             g = a * PACK + i
-            bank = rps.tile([P, HALF], F32, name="rbank")
+            bank = psum.tile([P, HALF], F32, name="rbank", tag="bank")
             nc.tensor.matmul_mx(
                 bank[:],
                 lhsT=w2_codes[:, g * 2 * P : (g + 1) * 2 * P].bitcast(E2M1X4),
@@ -164,46 +167,63 @@ def tile_list_camera_error_maps_kernel(tc, xT, wgt, offs, w1, gain, w2_words, w2
                 stop=True,
             )
             diff = ring.tile([P, HALF], F32, name="diff")
-            nc.vector.tensor_tensor(diff[:], bank[:], xg[a][h][:, i, :], ALU.subtract)
             err = ring.tile([P, HALF], F32, name="err", bufs=8)
-            nc.scalar.activation(err[:], diff[:], ACT.Square, scale=prec_sb[:, a, i : i + 1])
-            nc.sync.dma_start(out_planes[a, i][:, h * HALF : (h + 1) * HALF], err[:])
+            for c0 in range(0, HALF, step):
+                cols = slice(c0, c0 + step)
+                nc.vector.tensor_tensor(diff[:, cols], bank[:, cols], xg[a][:, i, h * HALF + c0 : h * HALF + c0 + step], ALU.subtract)
+                nc.scalar.activation(err[:, cols], diff[:, cols], ACT.Square, scale=prec_sb[:, a, i : i + 1])
+                nc.sync.dma_start(out_planes[a, i][:, h * HALF + c0 : h * HALF + c0 + step], err[:, cols])
 
-        for i in range(PACK):
-            for h in range(2):
-                gather(0, i, h)
-        for a in range(PASSES):
-            nc.scalar.copy(*w1_views(a))
-            weave_x(0, a, 0, HALF)
-        for a in range(PASSES):
-            quant_w1(a)
-            quant_x(0, a, 0, HALF)
-        for i in range(PACK):
-            gather(1, i, 0)
-        for c in range(2):
-            weave_x(1, 0, c * QUARTER, QUARTER)
-            quant_x(1, 0, c * QUARTER, QUARTER)
-        for i in range(PACK):
-            gather(1, i, 1)
+        for h in range(2):
+            gather(0, 0, h * HALF, HALF)
+        for i in range(1, PACK):
+            gather(0, i, 0, S)
+        weave_x(0, 0, S, nc.scalar.copy)
+        for i in range(2):
+            gather(1, i, 0, S)
+        quant_x(0, 0, S)
+        nc.scalar.copy(*w1_views(1))
+        quant_w1(1)
+        nc.scalar.copy(*w1_views(0))
+        gather(1, 2, 0, S)
+        quant_w1(0)
+        gather(1, 3, 0, QUARTER)
+        for b in range(S // N1):
+            encode_pass(b, 0, 0)
+        pieces = [(0, N1), (N1, N1), (QUARTER, QUARTER), (2 * QUARTER, QUARTER), (3 * QUARTER, QUARTER)]
+        weave_x(1, *pieces[0], nc.scalar.copy)
+        weave_x(1, *pieces[1], nc.scalar.copy)
+        gather(1, 3, QUARTER, QUARTER)
+        quant_x(1, *pieces[0])
         encode(0)
+        weave_x(1, *pieces[2], nc.scalar.copy)
+        quant_x(1, *pieces[1])
         encode(1)
-        for c in range(2):
-            weave_x(1, 1, c * QUARTER, QUARTER)
-        apply_gain(0)
-        apply_gain(1)
-        quant_x(1, 1, 0, QUARTER)
-        quant_h(0)
-        quant_x(1, 1, QUARTER, QUARTER)
+        gather(1, 3, HALF, HALF)
+        quant_x(1, *pieces[2])
         encode(2)
-        for g in range(4):
-            decode(0, 0, g)
         encode(3)
-        apply_gain(2)
+        apply_gain(*pieces[0])
+        apply_gain(*pieces[1])
+        weave_x(1, *pieces[3], nc.scalar.copy)
+        quant_x(1, *pieces[3])
+        apply_gain(*pieces[2])
+        weave_x(1, *pieces[4], nc.scalar.copy)
+        quant_h(0)
+        quant_x(1, *pieces[4])
+        encode(4)
+        encode(5)
+        decode(0, 0, 0)
+        decode(0, 0, 1)
+        encode(6)
+        encode(7)
+        apply_gain(*pieces[3])
+        decode(0, 0, 2)
+        decode(0, 0, 3)
+        apply_gain(*pieces[4])
         decode(0, 1, 0)
-        apply_gain(3)
-        decode(0, 1, 1)
         quant_h(1)
-        decode(0, 1, 2)
-        decode(0, 1, 3)
+        for i in range(1, PACK):
+            decode(0, 1, i)
         for g in range(PASSES * PACK):
-            decode(1, g // PACK, g % PACK)
+            decode(1, g // PACK, g % PACK, QUARTER if g == PASSES * PACK - 1 else HALF)

@@ -43,18 +43,17 @@ def tile_list_camera_error_maps_kernel(tc, xT, wgt, offs, w1, gain, w2_words, w2
         w2_plane = keep.tile([P, K], U8, name="w2_plane", align_bytes=64)
         wgt_sb = keep.tile([P, S], F32, name="wgt_sb")
         x_sb = [[keep.tile([P, T], F32, name="x%d%d" % (a, i), align_bytes=64) for i in range(PACK)] for a in range(PASSES)]
-        w1_raw = [keep.tile([P, PACK, H], F32, name="w1raw%d" % a) for a in range(PASSES)]
+        w1_raw = {(1, 0): keep.tile([P, PACK, H], F32, name="w1raw1"), (0, 0): keep.tile([P, 2, H], F32, name="w1raw00"), (0, 2): keep.tile([P, 2, H], F32, name="w1raw02")}
         gain_sb = keep.tile([P, PACK], F32, name="gain_sb")
         prec_sb = keep.tile([P, PASSES, PACK], F32, name="prec_sb")
         warm = keep.tile([P, 1], F32, name="warm")
 
-        xg = [keep.tile([P, PACK, S], F32, name="xg%d" % a) for a in range(PASSES)]
+        xg = [keep.tile([P, PACK, S], F32, name="xg%d" % a, align_bytes=64) for a in range(PASSES)]
         xb = [keep.tile([P, S * PACK], BF16, name="xb%d" % a, align_bytes=64) for a in range(PASSES)]
-        after_x11 = keep.tile([P, S + H], U32, name="after_x11", tag="x11", align_bytes=64)
-        x_codes = [after_x11[:, 0:S], keep.tile([P, S], U32, name="xc1", align_bytes=64)]
+        x_codes = [keep.tile([P, S], U32, name="xc0", tag="x11", align_bytes=64), keep.tile([P, S], U32, name="xc1", align_bytes=64)]
         x_plane = [keep.tile([P, S], U8, name="xs%d" % a, align_bytes=64) for a in range(PASSES)]
         w1b = [keep.tile([P, H * PACK], BF16, name="w1b%d" % a, align_bytes=64) for a in range(PASSES)]
-        w1_codes = [keep.tile([P, H], U32, name="w1c0", align_bytes=64), after_x11[:, S : S + H]]
+        w1_codes = [keep.tile([P, H], U32, name="w1c%d" % a, align_bytes=64) for a in range(PASSES)]
         w1_plane = [keep.tile([P, H], U8, name="w1s%d" % a, align_bytes=64) for a in range(PASSES)]
         th = keep.tile([P, S * PACK], F32, name="th")
         hb = [keep.tile([P, HALF * PACK], BF16, name="hb%d" % h, align_bytes=64) for h in range(2)]
@@ -74,13 +73,15 @@ def tile_list_camera_error_maps_kernel(tc, xT, wgt, offs, w1, gain, w2_words, w2
         nc.sync.dma_start(wgt_sb[:, HALF:S], wgt[:, HALF:S])
         for i in range(1, PACK):
             nc.sync.dma_start(x_sb[0][i][:], x_planes[0, i])
-        nc.sync.dma_start(gain_sb[:], gain.rearrange("(p t) -> p t", t=PACK))
-        nc.sync.dma_start(prec_sb[:], prec.rearrange("(a p i) -> p a i", a=PASSES, i=PACK))
         for i in range(2):
             nc.sync.dma_start(x_sb[1][i][:], x_planes[1, i])
-        for i in range(2):
-            nc.sync.dma_start(w1_raw[1 - i][:], w1_rows[1 - i])
-            nc.sync.dma_start(x_sb[1][2 + i][:], x_planes[1, 2 + i])
+        nc.sync.dma_start(w1_raw[1, 0][:], w1_rows[1])
+        nc.sync.dma_start(w1_raw[0, 0][:], w1_rows[0][:, 0:2, :])
+        nc.sync.dma_start(x_sb[1][2][:], x_planes[1, 2])
+        nc.sync.dma_start(w1_raw[0, 2][:], w1_rows[0][:, 2:4, :])
+        nc.sync.dma_start(x_sb[1][PACK - 1][:], x_planes[1, PACK - 1])
+        nc.sync.dma_start(gain_sb[:], gain.rearrange("(p t) -> p t", t=PACK))
+        nc.sync.dma_start(prec_sb[:], prec.rearrange("(a p i) -> p a i", a=PASSES, i=PACK))
 
         nc.vector.tensor_copy(
             w2_codes[:].rearrange("p (a i q b) -> p a i q b", a=PASSES, i=PACK, b=2),
@@ -95,9 +96,14 @@ def tile_list_camera_error_maps_kernel(tc, xT, wgt, offs, w1, gain, w2_words, w2
             window = x_sb[a][i][:].indirect(offsets[:, c0 // 16 : (c0 + n) // 16])
             nc.vector.tensor_tensor(xg[a][:, i, c0 : c0 + n], window, wgt_sb[:, c0 : c0 + n], ALU.mult)
 
+        def woven(a, c0, n):
+            if a == 1 and c0 < QUARTER:
+                return xg[1][:, PACK - 1, HALF + 2 * c0 : HALF + 2 * (c0 + n)].bitcast(BF16)
+            return xb[a][:, c0 * PACK : (c0 + n) * PACK]
+
         def weave_x(a, c0, n, copy):
             copy(
-                xb[a][:, c0 * PACK : (c0 + n) * PACK].rearrange("p (c e i) -> p c i e", e=LINE, i=PACK),
+                woven(a, c0, n).rearrange("p (c e i) -> p c i e", e=LINE, i=PACK),
                 xg[a][:, :, c0 : c0 + n].rearrange("p i (c e) -> p c i e", e=LINE),
             )
 
@@ -105,13 +111,19 @@ def tile_list_camera_error_maps_kernel(tc, xT, wgt, offs, w1, gain, w2_words, w2
             nc.vector.quantize_mx(
                 x_codes[a][:, c0 : c0 + n].bitcast(E4M3X4),
                 x_plane[a][:, c0 : c0 + n],
-                xb[a][:, c0 * PACK : (c0 + n) * PACK],
+                woven(a, c0, n),
             )
 
-        def w1_views(a):
-            return (
-                w1b[a][:].rearrange("p (t m i) -> p m i t", t=PACK, i=PACK),
-                w1_raw[a][:].rearrange("p i (m t) -> p m i t", t=PACK),
+        def weave_x_pair(i0):
+            nc.scalar.copy(
+                xb[0][:].rearrange("p (c i) -> p c i", i=PACK)[:, :, i0 : i0 + 2],
+                xg[0][:, i0 : i0 + 2, :].rearrange("p i c -> p c i"),
+            )
+
+        def cast_w1(a, i0, n):
+            nc.scalar.copy(
+                w1b[a][:].rearrange("p (t m i) -> p m i t", t=PACK, i=PACK)[:, :, i0 : i0 + n, :],
+                w1_raw[a, i0][:].rearrange("p i (m t) -> p m i t", t=PACK),
             )
 
         def quant_w1(a):
@@ -141,10 +153,10 @@ def tile_list_camera_error_maps_kernel(tc, xT, wgt, offs, w1, gain, w2_words, w2
                 ACT.Tanh,
             )
 
-        def apply_gain(c0, n):
+        def apply_gain(c0, n, engine=nc.vector):
             h = c0 // HALF
             o = (c0 - h * HALF) * PACK
-            nc.vector.tensor_tensor(
+            engine.tensor_tensor(
                 hb[h][:, o : o + n * PACK].rearrange("p (n t) -> p n t", t=PACK),
                 th[:, c0 * PACK : (c0 + n) * PACK].rearrange("p (n t) -> p n t", t=PACK),
                 gain_sb[:].unsqueeze(1).to_broadcast([P, n, PACK]),
@@ -178,49 +190,45 @@ def tile_list_camera_error_maps_kernel(tc, xT, wgt, offs, w1, gain, w2_words, w2
             gather(0, 0, h * HALF, HALF)
         for i in range(1, PACK):
             gather(0, i, 0, S)
-        weave_x(0, 0, S, nc.scalar.copy)
+            if i % 2 == 1:
+                weave_x_pair(i - 1)
         for i in range(2):
             gather(1, i, 0, S)
         quant_x(0, 0, S)
-        nc.scalar.copy(*w1_views(1))
+        cast_w1(1, 0, PACK)
         quant_w1(1)
-        nc.scalar.copy(*w1_views(0))
+        cast_w1(0, 0, 2)
         gather(1, 2, 0, S)
+        cast_w1(0, 2, 2)
         quant_w1(0)
-        gather(1, 3, 0, QUARTER)
         for b in range(S // N1):
             encode_pass(b, 0, 0)
         pieces = [(0, N1), (N1, N1), (QUARTER, QUARTER), (2 * QUARTER, QUARTER), (3 * QUARTER, QUARTER)]
-        weave_x(1, *pieces[0], nc.scalar.copy)
-        weave_x(1, *pieces[1], nc.scalar.copy)
-        gather(1, 3, QUARTER, QUARTER)
-        quant_x(1, *pieces[0])
-        encode(0)
-        weave_x(1, *pieces[2], nc.scalar.copy)
-        quant_x(1, *pieces[1])
-        encode(1)
+        for k in range(3):
+            gather(1, 3, *pieces[k])
+        for k in range(2):
+            weave_x(1, *pieces[k], nc.scalar.copy)
+            quant_x(1, *pieces[k])
+            encode(k)
         gather(1, 3, HALF, HALF)
+        weave_x(1, *pieces[2], nc.scalar.copy)
         quant_x(1, *pieces[2])
         encode(2)
         encode(3)
-        apply_gain(*pieces[0])
-        apply_gain(*pieces[1])
-        weave_x(1, *pieces[3], nc.scalar.copy)
-        quant_x(1, *pieces[3])
-        apply_gain(*pieces[2])
-        weave_x(1, *pieces[4], nc.scalar.copy)
+        for k in range(3):
+            apply_gain(*pieces[k])
+        for k in range(3, 5):
+            weave_x(1, *pieces[k], nc.scalar.copy)
+            quant_x(1, *pieces[k])
+            encode(2 * k - 2)
+            encode(2 * k - 1)
         quant_h(0)
-        quant_x(1, *pieces[4])
-        encode(4)
-        encode(5)
         decode(0, 0, 0)
         decode(0, 0, 1)
-        encode(6)
-        encode(7)
         apply_gain(*pieces[3])
         decode(0, 0, 2)
         decode(0, 0, 3)
-        apply_gain(*pieces[4])
+        apply_gain(*pieces[4], engine=nc.gpsimd)
         decode(0, 1, 0)
         quant_h(1)
         for i in range(1, PACK):

@@ -28,12 +28,11 @@ LINE = 4
 def tile_list_camera_error_maps_kernel(tc, xT, wgt, offs, w1, gain, w2_words, w2_scales, prec, out):
     nc = tc.nc
     x_planes = xT.rearrange("(a p i) t -> a i p t", a=PASSES, i=PACK)
-    out_planes = out.rearrange("(a p i) j -> a i p j", a=PASSES, i=PACK)
+    out_rows = out.rearrange("(a p i) j -> a p i j", a=PASSES, i=PACK)
     w1_rows = w1.rearrange("(a p i) r -> a p i r", a=PASSES, i=PACK)
 
     with ExitStack() as ctx:
         keep = ctx.enter_context(tc.tile_pool(name="keep", bufs=1))
-        ring = ctx.enter_context(tc.tile_pool(name="ring", bufs=4))
         psum = ctx.enter_context(tc.psum_pool(name="psum", bufs=8))
 
         offsets = keep.tile([P, S // 16], U16, name="offsets")
@@ -43,87 +42,104 @@ def tile_list_camera_error_maps_kernel(tc, xT, wgt, offs, w1, gain, w2_words, w2
         w2_plane = keep.tile([P, K], U8, name="w2_plane", align_bytes=64)
         wgt_sb = keep.tile([P, S], F32, name="wgt_sb")
         x_sb = [[keep.tile([P, T], F32, name="x%d%d" % (a, i), align_bytes=64) for i in range(PACK)] for a in range(PASSES)]
-        w1_raw = {(1, 0): keep.tile([P, PACK, H], F32, name="w1raw1"), (0, 0): keep.tile([P, 2, H], F32, name="w1raw00"), (0, 2): keep.tile([P, 2, H], F32, name="w1raw02")}
+        w1_parts = [(0, 0, H - N1), (0, H - N1, N1), (1, 0, H // 2), (1, H // 2, H // 2)]
         gain_sb = keep.tile([P, PACK], F32, name="gain_sb")
         prec_sb = keep.tile([P, PASSES, PACK], F32, name="prec_sb")
-        warm = keep.tile([P, 1], F32, name="warm")
 
         xg = [keep.tile([P, PACK, S], F32, name="xg%d" % a, align_bytes=64) for a in range(PASSES)]
-        xb = [keep.tile([P, S * PACK], BF16, name="xb%d" % a, align_bytes=64) for a in range(PASSES)]
+        w1_raw = [
+            keep.tile([P, PACK, H - N1], F32, name="w1raw0", align_bytes=64)[:],
+            xg[1][:, PACK - 1, HALF:S].rearrange("p (i r) -> p i r", i=PACK),
+            keep.tile([P, PACK, H // 2], F32, name="w1raw2", align_bytes=64)[:],
+            keep.tile([P, PACK, H // 2], F32, name="w1raw3", align_bytes=64)[:],
+        ]
+        xb = [keep.tile([P, S * PACK], BF16, name="xb0", align_bytes=64), keep.tile([P, (S - QUARTER) * PACK], BF16, name="xb1", tag="w1raw2", align_bytes=64)]
         x_codes = [keep.tile([P, S], U32, name="xc0", tag="x11", align_bytes=64), keep.tile([P, S], U32, name="xc1", align_bytes=64)]
         x_plane = [keep.tile([P, S], U8, name="xs%d" % a, align_bytes=64) for a in range(PASSES)]
         w1b = [keep.tile([P, H * PACK], BF16, name="w1b%d" % a, align_bytes=64) for a in range(PASSES)]
         w1_codes = [keep.tile([P, H], U32, name="w1c%d" % a, align_bytes=64) for a in range(PASSES)]
         w1_plane = [keep.tile([P, H], U8, name="w1s%d" % a, align_bytes=64) for a in range(PASSES)]
         th = keep.tile([P, S * PACK], F32, name="th")
-        hb = [keep.tile([P, HALF * PACK], BF16, name="hb%d" % h, align_bytes=64) for h in range(2)]
-        h_codes = [keep.tile([P, HALF], U32, name="hc%d" % h, align_bytes=64) for h in range(2)]
-        h_plane = [keep.tile([P, HALF], U8, name="hs%d" % h, align_bytes=64) for h in range(2)]
+        hb = keep.tile([P, HALF * PACK], BF16, name="hb", align_bytes=64)
+        h_codes = keep.tile([P, S], U32, name="hc", align_bytes=64)
+        h_plane = keep.tile([P, S], U8, name="hs", align_bytes=64)
 
-        nc.gpsimd.memset(s2_raw[:].bitcast(U32), 0)
-        nc.gpsimd.memset(warm[:], 0.0)
+        nc.vector.memset(s2_raw[:].bitcast(U32), 0)
+        def load_x(a, i):
+            nc.sync.dma_start(x_sb[a][i][:], x_planes[a, i])
+
+        def load_w1(k):
+            a, r0, n = w1_parts[k]
+            nc.sync.dma_start(w1_raw[k], w1_rows[a][:, :, r0 : r0 + n])
+
         nc.sync.dma_start(offsets[:], offs)
         nc.sync.dma_start(w2_raw[:].bitcast(I32), w2_words[0].bitcast(I32))
         nc.sync.dma_start(wgt_sb[:, 0:HALF], wgt[:, 0:HALF])
-        nc.sync.dma_start(x_sb[0][0][:], x_planes[0, 0])
-        scale_rows = w2_scales[0].bitcast(I32)
-        for q in range(4):
-            nc.sync.dma_start(s2_raw[32 * q : 32 * q + 4, :].bitcast(I32), scale_rows[4 * q : 4 * q + 4, :])
-        nc.scalar.activation(warm[:], warm[:], ACT.Tanh)
+        scale_rows = w2_scales[0].bitcast(I32).rearrange("(q r) c -> r q c", r=4)
+        for r in range(4):
+            nc.sync.dma_start(s2_raw[r:P:32, :].bitcast(I32), scale_rows[r])
+        load_x(0, 0)
         nc.sync.dma_start(wgt_sb[:, HALF:S], wgt[:, HALF:S])
-        for i in range(1, PACK):
-            nc.sync.dma_start(x_sb[0][i][:], x_planes[0, i])
-        for i in range(2):
-            nc.sync.dma_start(x_sb[1][i][:], x_planes[1, i])
-        nc.sync.dma_start(w1_raw[1, 0][:], w1_rows[1])
-        nc.sync.dma_start(w1_raw[0, 0][:], w1_rows[0][:, 0:2, :])
-        nc.sync.dma_start(x_sb[1][2][:], x_planes[1, 2])
-        nc.sync.dma_start(w1_raw[0, 2][:], w1_rows[0][:, 2:4, :])
-        nc.sync.dma_start(x_sb[1][PACK - 1][:], x_planes[1, PACK - 1])
+        load_x(0, 1)
+        load_x(0, 2)
+        load_x(0, 3)
+        load_x(1, 0)
+        load_x(1, 1)
+        load_w1(0)
+        load_w1(1)
+        load_w1(2)
+        load_w1(3)
+        load_x(1, 2)
+        load_x(1, 3)
         nc.sync.dma_start(gain_sb[:], gain.rearrange("(p t) -> p t", t=PACK))
         nc.sync.dma_start(prec_sb[:], prec.rearrange("(a p i) -> p a i", a=PASSES, i=PACK))
 
-        nc.vector.tensor_copy(
-            w2_codes[:].rearrange("p (a i q b) -> p a i q b", a=PASSES, i=PACK, b=2),
-            w2_raw[:].rearrange("p (a q i b) -> p a i q b", a=PASSES, i=PACK, b=2),
-        )
-        nc.vector.tensor_copy(
-            w2_plane[:].rearrange("p (a i q) -> p a i q", a=PASSES, i=PACK),
-            s2_raw[:].rearrange("p (a q i) -> p a i q", a=PASSES, i=PACK),
-        )
+        def deal_w2_words():
+            nc.vector.tensor_copy(
+                w2_codes[:].bitcast(U16).rearrange("p (a i q) -> p a i q", a=PASSES, i=PACK),
+                w2_raw[:].bitcast(U16).rearrange("p (a q i) -> p a i q", a=PASSES, i=PACK),
+            )
+
+        def deal_w2_scales():
+            nc.vector.tensor_copy(
+                w2_plane[:].rearrange("p (a i q) -> p a i q", a=PASSES, i=PACK),
+                s2_raw[:].rearrange("p (a q i) -> p a i q", a=PASSES, i=PACK),
+            )
+
+        chunks = [(0, N1), (N1, N1), (QUARTER, QUARTER), (2 * QUARTER, QUARTER), (3 * QUARTER, QUARTER)]
 
         def gather(a, i, c0, n):
             window = x_sb[a][i][:].indirect(offsets[:, c0 // 16 : (c0 + n) // 16])
             nc.vector.tensor_tensor(xg[a][:, i, c0 : c0 + n], window, wgt_sb[:, c0 : c0 + n], ALU.mult)
 
         def woven(a, c0, n):
-            if a == 1 and c0 < QUARTER:
+            if a == 0:
+                return xb[0][:, c0 * PACK : (c0 + n) * PACK]
+            if c0 < QUARTER:
                 return xg[1][:, PACK - 1, HALF + 2 * c0 : HALF + 2 * (c0 + n)].bitcast(BF16)
-            return xb[a][:, c0 * PACK : (c0 + n) * PACK]
+            return xb[1][:, (c0 - QUARTER) * PACK : (c0 - QUARTER + n) * PACK]
 
-        def weave_x(a, c0, n, copy):
+        def weave_pair(a, i0, c0, n, copy):
             copy(
-                woven(a, c0, n).rearrange("p (c e i) -> p c i e", e=LINE, i=PACK),
-                xg[a][:, :, c0 : c0 + n].rearrange("p i (c e) -> p c i e", e=LINE),
+                woven(a, c0, n).rearrange("p (c i) -> p c i", i=PACK)[:, :, i0 : i0 + 2],
+                xg[a][:, i0 : i0 + 2, c0 : c0 + n].rearrange("p i c -> p c i"),
             )
+
+        def codes_x(a, c0, n):
+            return x_codes[a][:, c0 : c0 + n].bitcast(E4M3X4)
 
         def quant_x(a, c0, n):
             nc.vector.quantize_mx(
-                x_codes[a][:, c0 : c0 + n].bitcast(E4M3X4),
+                codes_x(a, c0, n),
                 x_plane[a][:, c0 : c0 + n],
                 woven(a, c0, n),
             )
 
-        def weave_x_pair(i0):
-            nc.scalar.copy(
-                xb[0][:].rearrange("p (c i) -> p c i", i=PACK)[:, :, i0 : i0 + 2],
-                xg[0][:, i0 : i0 + 2, :].rearrange("p i c -> p c i"),
-            )
-
-        def cast_w1(a, i0, n):
-            nc.scalar.copy(
-                w1b[a][:].rearrange("p (t m i) -> p m i t", t=PACK, i=PACK)[:, :, i0 : i0 + n, :],
-                w1_raw[a, i0][:].rearrange("p i (m t) -> p m i t", t=PACK),
+        def cast_w1(k, copy=nc.scalar.copy):
+            a, r0, n = w1_parts[k]
+            copy(
+                w1b[a][:].rearrange("p (t m i) -> p m i t", t=PACK, i=PACK)[:, r0 // PACK : (r0 + n) // PACK, :, :],
+                w1_raw[k].rearrange("p i (m t) -> p m i t", t=PACK),
             )
 
         def quant_w1(a):
@@ -131,107 +147,131 @@ def tile_list_camera_error_maps_kernel(tc, xT, wgt, offs, w1, gain, w2_words, w2
 
         banks = [psum.tile([P, PACK, N1], F32, name="hbank%d" % b, tag="bank") for b in range(S // N1)]
 
-        def encode_pass(b, t, a):
-            nc.tensor.matmul_mx(
-                banks[b][:, t, :],
-                lhsT=w1_codes[a][:, t * P : (t + 1) * P].bitcast(E4M3X4),
-                lhsT_scale=w1_plane[a][:, t * P : (t + 1) * P],
-                rhs=x_codes[a][:, b * N1 : (b + 1) * N1].bitcast(E4M3X4),
-                rhs_scale=x_plane[a][:, b * N1 : (b + 1) * N1],
-                start=(a == 0),
-                stop=(a == PASSES - 1),
-            )
-
-        def encode(b):
+        def encode_pass(b, a):
             for t in range(PACK):
-                for a in range(PASSES):
-                    if (t, a) != (0, 0):
-                        encode_pass(b, t, a)
-            nc.scalar.activation(
-                th[:, b * N1 * PACK : (b + 1) * N1 * PACK].rearrange("p (n t) -> p n t", t=PACK),
-                banks[b][:].rearrange("p t n -> p n t"),
-                ACT.Tanh,
-            )
+                nc.tensor.matmul_mx(
+                    banks[b][:, t, :],
+                    lhsT=w1_codes[a][:, t * P : (t + 1) * P].bitcast(E4M3X4),
+                    lhsT_scale=w1_plane[a][:, t * P : (t + 1) * P],
+                    rhs=codes_x(a, b * N1, N1),
+                    rhs_scale=x_plane[a][:, b * N1 : (b + 1) * N1],
+                    start=(a == 0 and t == 0),
+                    stop=(a == PASSES - 1 and t == PACK - 1),
+                )
 
-        def apply_gain(c0, n, engine=nc.vector):
-            h = c0 // HALF
-            o = (c0 - h * HALF) * PACK
+        def encode(c0, n):
+            for b in range(c0 // N1, (c0 + n) // N1):
+                encode_pass(b, 1)
+                nc.scalar.activation(
+                    th[:, b * N1 * PACK : (b + 1) * N1 * PACK].rearrange("p (n t) -> p n t", t=PACK),
+                    banks[b][:].rearrange("p t n -> p n t"),
+                    ACT.Tanh,
+                )
+
+        def rounded_h(c0, n):
+            first = min(c0, QUARTER) * PACK
+            return hb[:, first : first + n * PACK]
+
+        def apply_gain(c0, n, engine):
             engine.tensor_tensor(
-                hb[h][:, o : o + n * PACK].rearrange("p (n t) -> p n t", t=PACK),
+                rounded_h(c0, n).rearrange("p (n t) -> p n t", t=PACK),
                 th[:, c0 * PACK : (c0 + n) * PACK].rearrange("p (n t) -> p n t", t=PACK),
                 gain_sb[:].unsqueeze(1).to_broadcast([P, n, PACK]),
                 ALU.mult,
             )
 
-        def quant_h(h):
-            nc.vector.quantize_mx(h_codes[h][:].bitcast(E4M3X4), h_plane[h][:], hb[h][:])
+        def quant_h(c0, n):
+            nc.vector.quantize_mx(h_codes[:, c0 : c0 + n].bitcast(E4M3X4), h_plane[:, c0 : c0 + n], rounded_h(c0, n))
 
-        def decode(h, a, i, step=HALF):
-            g = a * PACK + i
-            bank = psum.tile([P, HALF], F32, name="rbank", tag="bank")
-            nc.tensor.matmul_mx(
-                bank[:],
-                lhsT=w2_codes[:, g * 2 * P : (g + 1) * 2 * P].bitcast(E2M1X4),
-                lhsT_scale=w2_plane[:, g * P : (g + 1) * P],
-                rhs=h_codes[h][:].bitcast(E4M3X4),
-                rhs_scale=h_plane[h][:],
-                start=True,
-                stop=True,
-            )
-            diff = ring.tile([P, HALF], F32, name="diff")
-            err = ring.tile([P, HALF], F32, name="err", bufs=8)
-            for c0 in range(0, HALF, step):
-                cols = slice(c0, c0 + step)
-                nc.vector.tensor_tensor(diff[:, cols], bank[:, cols], xg[a][:, i, h * HALF + c0 : h * HALF + c0 + step], ALU.subtract)
-                nc.scalar.activation(err[:, cols], diff[:, cols], ACT.Square, scale=prec_sb[:, a, i : i + 1])
-                nc.sync.dma_start(out_planes[a, i][:, h * HALF + c0 : h * HALF + c0 + step], err[:, cols])
+        def difference(c0, n, a):
+            return xg[a][:, :, c0 : c0 + n]
 
+        def decode(c0, n, a):
+            cols = slice(c0, c0 + n)
+            per_bank = HALF // n
+            for j0 in range(0, PACK, per_bank):
+                bank = psum.tile([P, per_bank, n], F32, name="rbank", tag="bank")
+                for u in range(per_bank):
+                    g = a * PACK + j0 + u
+                    nc.tensor.matmul_mx(
+                        bank[:, u, :],
+                        lhsT=w2_codes[:, g * 2 * P : (g + 1) * 2 * P].bitcast(E2M1X4),
+                        lhsT_scale=w2_plane[:, g * P : (g + 1) * P],
+                        rhs=h_codes[:, cols].bitcast(E4M3X4),
+                        rhs_scale=h_plane[:, cols],
+                        start=True,
+                        stop=True,
+                    )
+                nc.vector.tensor_tensor(difference(c0, n, a)[:, j0 : j0 + per_bank, :], bank[:], xg[a][:, j0 : j0 + per_bank, cols], ALU.subtract)
+
+        def finish(c0, n, a, i0=0, count=PACK):
+            cols = slice(c0, c0 + n)
+            for i in range(i0, i0 + count):
+                nc.scalar.activation(xg[a][:, i, cols], difference(c0, n, a)[:, i, :], ACT.Square, scale=prec_sb[:, a, i : i + 1])
+            nc.sync.dma_start(out_rows[a][:, i0 : i0 + count, cols], xg[a][:, i0 : i0 + count, cols])
+
+        deal_w2_words()
+        deal_w2_scales()
         for h in range(2):
             gather(0, 0, h * HALF, HALF)
-        for i in range(1, PACK):
-            gather(0, i, 0, S)
-            if i % 2 == 1:
-                weave_x_pair(i - 1)
+        gather(0, 1, 0, S)
+        weave_pair(0, 0, 0, S, nc.scalar.copy)
+        gather(0, 2, 0, S)
+        for h in range(2):
+            gather(0, 3, h * HALF, HALF)
+            weave_pair(0, 2, h * HALF, HALF, nc.scalar.copy)
+        cast_w1(0)
+        cast_w1(1)
         for i in range(2):
             gather(1, i, 0, S)
         quant_x(0, 0, S)
-        cast_w1(1, 0, PACK)
-        quant_w1(1)
-        cast_w1(0, 0, 2)
-        gather(1, 2, 0, S)
-        cast_w1(0, 2, 2)
         quant_w1(0)
+        weave_pair(1, 0, 0, QUARTER, nc.scalar.copy)
+        cast_w1(2)
+        weave_pair(1, 0, QUARTER, S - QUARTER, nc.scalar.copy)
+        cast_w1(3, nc.vector.tensor_copy)
         for b in range(S // N1):
-            encode_pass(b, 0, 0)
-        pieces = [(0, N1), (N1, N1), (QUARTER, QUARTER), (2 * QUARTER, QUARTER), (3 * QUARTER, QUARTER)]
+            encode_pass(b, 0)
+        quant_w1(1)
+        gather(1, 2, 0, S)
         for k in range(3):
-            gather(1, 3, *pieces[k])
+            gather(1, 3, *chunks[k])
+            weave_pair(1, 2, *chunks[k], nc.scalar.copy)
         for k in range(2):
-            weave_x(1, *pieces[k], nc.scalar.copy)
-            quant_x(1, *pieces[k])
-            encode(k)
-        gather(1, 3, HALF, HALF)
-        weave_x(1, *pieces[2], nc.scalar.copy)
-        quant_x(1, *pieces[2])
-        encode(2)
-        encode(3)
-        for k in range(3):
-            apply_gain(*pieces[k])
-        for k in range(3, 5):
-            weave_x(1, *pieces[k], nc.scalar.copy)
-            quant_x(1, *pieces[k])
-            encode(2 * k - 2)
-            encode(2 * k - 1)
-        quant_h(0)
-        decode(0, 0, 0)
-        decode(0, 0, 1)
-        apply_gain(*pieces[3])
-        decode(0, 0, 2)
-        decode(0, 0, 3)
-        apply_gain(*pieces[4], engine=nc.gpsimd)
-        decode(0, 1, 0)
-        quant_h(1)
-        for i in range(1, PACK):
-            decode(0, 1, i)
-        for g in range(PASSES * PACK):
-            decode(1, g // PACK, g % PACK, QUARTER if g == PASSES * PACK - 1 else HALF)
+            quant_x(1, *chunks[k])
+            encode(*chunks[k])
+            gather(1, 3, *chunks[k + 3])
+        weave_pair(1, 2, *chunks[3], nc.scalar.copy)
+        quant_x(1, *chunks[2])
+        apply_gain(*chunks[0], nc.vector)
+        weave_pair(1, 2, *chunks[4], nc.scalar.copy)
+        encode(*chunks[2])
+        apply_gain(*chunks[1], nc.vector)
+        quant_h(*chunks[0])
+        quant_x(1, HALF, HALF)
+        quant_h(*chunks[1])
+        encode(*chunks[3])
+        for a in range(PASSES):
+            decode(*chunks[0], a)
+            finish(*chunks[0], a)
+        encode(*chunks[4])
+        apply_gain(*chunks[2], nc.vector)
+        quant_h(*chunks[2])
+        apply_gain(*chunks[3], nc.gpsimd)
+        for a in range(PASSES):
+            decode(*chunks[1], a)
+            finish(*chunks[1], a)
+        for k in range(2, 4):
+            decode(*chunks[k], 0)
+            finish(*chunks[k], 0)
+            quant_h(*chunks[k + 1])
+            if k == 2:
+                apply_gain(*chunks[4], nc.gpsimd)
+            decode(*chunks[k], 1)
+            finish(*chunks[k], 1)
+        decode(*chunks[4], 0)
+        finish(*chunks[4], 0)
+        decode(*chunks[4], 1)
+        finish(*chunks[4], 1, 0, 2)
+        finish(*chunks[4], 1, 2, 1)
+        finish(*chunks[4], 1, 3, 1)

@@ -1,6 +1,7 @@
 from contextlib import ExitStack
 
 import concourse.mybir as mybir
+from concourse.masks import make_identity
 
 K, T, S, H = 1024, 2048, 1024, 512
 FLOPS = 2 * 2 * K * H * S
@@ -22,7 +23,9 @@ PASSES = 2
 HALF = 512
 QUARTER = 256
 N1 = 128
-LINE = 4
+VECTOR_SHARE = 48
+CAMERAS = 8
+GROUP = 16
 
 
 def tile_list_camera_error_maps_kernel(tc, xT, wgt, offs, w1, gain, w2_words, w2_scales, prec, out):
@@ -41,18 +44,17 @@ def tile_list_camera_error_maps_kernel(tc, xT, wgt, offs, w1, gain, w2_words, w2
         w2_codes = keep.tile([P, 2 * K], U8, name="w2_codes", align_bytes=64)
         w2_plane = keep.tile([P, K], U8, name="w2_plane", align_bytes=64)
         wgt_sb = keep.tile([P, S], F32, name="wgt_sb")
+        wgt_rows = keep.tile([P, P], F32, name="wgt_rows")
+        wgt_spread = keep.tile([P, S], F32, name="wgt_spread")
+        identity = keep.tile([P, P], F32, name="identity")
         x_sb = [[keep.tile([P, T], F32, name="x%d%d" % (a, i), align_bytes=64) for i in range(PACK)] for a in range(PASSES)]
-        w1_parts = [(0, 0, H - N1), (0, H - N1, N1), (1, 0, H // 2), (1, H // 2, H // 2)]
+        w1_parts = [(0, 0, H // 2), (0, H // 2, H // 2), (1, 0, H - N1), (1, H - N1, N1)]
         gain_sb = keep.tile([P, PACK], F32, name="gain_sb")
         prec_sb = keep.tile([P, PASSES, PACK], F32, name="prec_sb")
 
         xg = [keep.tile([P, PACK, S], F32, name="xg%d" % a, align_bytes=64) for a in range(PASSES)]
-        w1_raw = [
-            keep.tile([P, PACK, H - N1], F32, name="w1raw0", align_bytes=64)[:],
-            xg[1][:, PACK - 1, HALF:S].rearrange("p (i r) -> p i r", i=PACK),
-            keep.tile([P, PACK, H // 2], F32, name="w1raw2", align_bytes=64)[:],
-            keep.tile([P, PACK, H // 2], F32, name="w1raw3", align_bytes=64)[:],
-        ]
+        w1_raw = [keep.tile([P, PACK, n], F32, name="w1raw%d" % k, align_bytes=64)[:] for k, (a, r0, n) in enumerate(w1_parts[:-1])]
+        w1_raw.append(xg[1][:, PACK - 1, HALF:S].rearrange("p (i r) -> p i r", i=PACK))
         xb = [keep.tile([P, S * PACK], BF16, name="xb0", align_bytes=64), keep.tile([P, (S - QUARTER) * PACK], BF16, name="xb1", tag="w1raw2", align_bytes=64)]
         x_codes = [keep.tile([P, S], U32, name="xc0", tag="x11", align_bytes=64), keep.tile([P, S], U32, name="xc1", align_bytes=64)]
         x_plane = [keep.tile([P, S], U8, name="xs%d" % a, align_bytes=64) for a in range(PASSES)]
@@ -64,6 +66,8 @@ def tile_list_camera_error_maps_kernel(tc, xT, wgt, offs, w1, gain, w2_words, w2
         h_codes = keep.tile([P, S], U32, name="hc", align_bytes=64)
         h_plane = keep.tile([P, S], U8, name="hs", align_bytes=64)
 
+        nc.vector.memset(wgt_rows[P // 2 : P, :], 0.0)
+        make_identity(nc, identity[:])
         nc.vector.memset(s2_raw[:].bitcast(U32), 0)
         def load_x(a, i):
             nc.sync.dma_start(x_sb[a][i][:], x_planes[a, i])
@@ -72,14 +76,13 @@ def tile_list_camera_error_maps_kernel(tc, xT, wgt, offs, w1, gain, w2_words, w2
             a, r0, n = w1_parts[k]
             nc.sync.dma_start(w1_raw[k], w1_rows[a][:, :, r0 : r0 + n])
 
+        nc.sync.dma_start(wgt_rows[0 : P // 2, :], wgt.rearrange("(g r) (c e) -> r g c e", r=GROUP, e=P)[0])
         nc.sync.dma_start(offsets[:], offs)
         nc.sync.dma_start(w2_raw[:].bitcast(I32), w2_words[0].bitcast(I32))
-        nc.sync.dma_start(wgt_sb[:, 0:HALF], wgt[:, 0:HALF])
         scale_rows = w2_scales[0].bitcast(I32).rearrange("(q r) c -> r q c", r=4)
         for r in range(4):
             nc.sync.dma_start(s2_raw[r:P:32, :].bitcast(I32), scale_rows[r])
         load_x(0, 0)
-        nc.sync.dma_start(wgt_sb[:, HALF:S], wgt[:, HALF:S])
         load_x(0, 1)
         load_x(0, 2)
         load_x(0, 3)
@@ -93,6 +96,22 @@ def tile_list_camera_error_maps_kernel(tc, xT, wgt, offs, w1, gain, w2_words, w2
         load_x(1, 3)
         nc.sync.dma_start(gain_sb[:], gain.rearrange("(p t) -> p t", t=PACK))
         nc.sync.dma_start(prec_sb[:], prec.rearrange("(a p i) -> p a i", a=PASSES, i=PACK))
+
+        def spread_wgt():
+            turned = psum.tile([P, P], F32, name="turned", tag="bank")
+            nc.tensor.transpose(turned[:], wgt_rows[:], identity[:])
+            per_bank = HALF // P
+            for h in range(2):
+                nc.scalar.copy(
+                    wgt_spread[:, h * HALF : (h + 1) * HALF].rearrange("p (c g r) -> p c g r", g=CAMERAS, r=GROUP),
+                    turned[:, 0 : P // 2].rearrange("p (g c) -> p c g", g=CAMERAS)[:, h * per_bank : (h + 1) * per_bank, :].unsqueeze(3).to_broadcast([P, per_bank, CAMERAS, GROUP]),
+                )
+            for h in range(2):
+                back = psum.tile([P, HALF], F32, name="back", tag="bank")
+                for c in range(per_bank):
+                    first = h * HALF + c * P
+                    nc.tensor.transpose(back[:, c * P : (c + 1) * P], wgt_spread[:, first : first + P], identity[:])
+                nc.scalar.copy(wgt_sb[:, h * HALF : (h + 1) * HALF], back[:])
 
         def deal_w2_words():
             nc.vector.tensor_copy(
@@ -145,7 +164,6 @@ def tile_list_camera_error_maps_kernel(tc, xT, wgt, offs, w1, gain, w2_words, w2
         def quant_w1(a):
             nc.vector.quantize_mx(w1_codes[a][:, 0:H].bitcast(E4M3X4), w1_plane[a][:], w1b[a][:])
 
-        banks = [psum.tile([P, PACK, N1], F32, name="hbank%d" % b, tag="bank") for b in range(S // N1)]
 
         def encode_pass(b, a):
             for t in range(PACK):
@@ -172,13 +190,18 @@ def tile_list_camera_error_maps_kernel(tc, xT, wgt, offs, w1, gain, w2_words, w2
             first = min(c0, QUARTER) * PACK
             return hb[:, first : first + n * PACK]
 
-        def apply_gain(c0, n, engine):
+        def apply_gain(c0, n, engine, skip=0, width=None):
+            width = n - skip if width is None else width
             engine.tensor_tensor(
-                rounded_h(c0, n).rearrange("p (n t) -> p n t", t=PACK),
-                th[:, c0 * PACK : (c0 + n) * PACK].rearrange("p (n t) -> p n t", t=PACK),
-                gain_sb[:].unsqueeze(1).to_broadcast([P, n, PACK]),
+                rounded_h(c0, n)[:, skip * PACK : (skip + width) * PACK].rearrange("p (n t) -> p n t", t=PACK),
+                th[:, (c0 + skip) * PACK : (c0 + skip + width) * PACK].rearrange("p (n t) -> p n t", t=PACK),
+                gain_sb[:].unsqueeze(1).to_broadcast([P, width, PACK]),
                 ALU.mult,
             )
+
+        def share_gain(c0, n):
+            apply_gain(c0, n, nc.vector, 0, VECTOR_SHARE)
+            apply_gain(c0, n, nc.gpsimd, VECTOR_SHARE)
 
         def quant_h(c0, n):
             nc.vector.quantize_mx(h_codes[:, c0 : c0 + n].bitcast(E4M3X4), h_plane[:, c0 : c0 + n], rounded_h(c0, n))
@@ -210,6 +233,8 @@ def tile_list_camera_error_maps_kernel(tc, xT, wgt, offs, w1, gain, w2_words, w2
                 nc.scalar.activation(xg[a][:, i, cols], difference(c0, n, a)[:, i, :], ACT.Square, scale=prec_sb[:, a, i : i + 1])
             nc.sync.dma_start(out_rows[a][:, i0 : i0 + count, cols], xg[a][:, i0 : i0 + count, cols])
 
+        spread_wgt()
+        banks = [psum.tile([P, PACK, N1], F32, name="hbank%d" % b, tag="bank") for b in range(S // N1)]
         deal_w2_words()
         deal_w2_scales()
         for h in range(2):
@@ -226,10 +251,10 @@ def tile_list_camera_error_maps_kernel(tc, xT, wgt, offs, w1, gain, w2_words, w2
             gather(1, i, 0, S)
         quant_x(0, 0, S)
         quant_w1(0)
-        weave_pair(1, 0, 0, QUARTER, nc.scalar.copy)
         cast_w1(2)
-        weave_pair(1, 0, QUARTER, S - QUARTER, nc.scalar.copy)
         cast_w1(3, nc.vector.tensor_copy)
+        weave_pair(1, 0, 0, QUARTER, nc.scalar.copy)
+        weave_pair(1, 0, QUARTER, S - QUARTER, nc.scalar.copy)
         for b in range(S // N1):
             encode_pass(b, 0)
         quant_w1(1)
@@ -250,27 +275,31 @@ def tile_list_camera_error_maps_kernel(tc, xT, wgt, offs, w1, gain, w2_words, w2
         quant_h(*chunks[0])
         quant_x(1, HALF, HALF)
         quant_h(*chunks[1])
+        decode(*chunks[0], 0)
+        finish(*chunks[0], 0)
         encode(*chunks[3])
-        for a in range(PASSES):
-            decode(*chunks[0], a)
-            finish(*chunks[0], a)
-        encode(*chunks[4])
         apply_gain(*chunks[2], nc.vector)
+        decode(*chunks[0], 1)
         quant_h(*chunks[2])
-        apply_gain(*chunks[3], nc.gpsimd)
+        finish(*chunks[0], 1)
+        share_gain(*chunks[3])
         for a in range(PASSES):
             decode(*chunks[1], a)
             finish(*chunks[1], a)
-        for k in range(2, 4):
-            decode(*chunks[k], 0)
-            finish(*chunks[k], 0)
-            quant_h(*chunks[k + 1])
-            if k == 2:
-                apply_gain(*chunks[4], nc.gpsimd)
-            decode(*chunks[k], 1)
-            finish(*chunks[k], 1)
-        decode(*chunks[4], 0)
-        finish(*chunks[4], 0)
+        encode(*chunks[4])
+        decode(*chunks[2], 0)
+        finish(*chunks[2], 0)
+        quant_h(*chunks[3])
+        share_gain(*chunks[4])
+        decode(*chunks[2], 1)
+        finish(*chunks[2], 1)
+        decode(*chunks[3], 0)
+        finish(*chunks[3], 0)
+        quant_h(*chunks[4])
+        for k, a in ((3, 1), (4, 0)):
+            decode(*chunks[k], a)
+            finish(*chunks[k], a, 0, 2)
+            finish(*chunks[k], a, 2, 2)
         decode(*chunks[4], 1)
         finish(*chunks[4], 1, 0, 2)
         finish(*chunks[4], 1, 2, 1)

@@ -23,7 +23,6 @@ PASSES = 2
 HALF = 512
 QUARTER = 256
 N1 = 128
-VECTOR_SHARE = 48
 CAMERAS = 8
 GROUP = 16
 
@@ -190,18 +189,13 @@ def tile_list_camera_error_maps_kernel(tc, xT, wgt, offs, w1, gain, w2_words, w2
             first = min(c0, QUARTER) * PACK
             return hb[:, first : first + n * PACK]
 
-        def apply_gain(c0, n, engine, skip=0, width=None):
-            width = n - skip if width is None else width
+        def apply_gain(c0, n, engine):
             engine.tensor_tensor(
-                rounded_h(c0, n)[:, skip * PACK : (skip + width) * PACK].rearrange("p (n t) -> p n t", t=PACK),
-                th[:, (c0 + skip) * PACK : (c0 + skip + width) * PACK].rearrange("p (n t) -> p n t", t=PACK),
-                gain_sb[:].unsqueeze(1).to_broadcast([P, width, PACK]),
+                rounded_h(c0, n).rearrange("p (n t) -> p n t", t=PACK),
+                th[:, c0 * PACK : (c0 + n) * PACK].rearrange("p (n t) -> p n t", t=PACK),
+                gain_sb[:].unsqueeze(1).to_broadcast([P, n, PACK]),
                 ALU.mult,
             )
-
-        def share_gain(c0, n):
-            apply_gain(c0, n, nc.vector, 0, VECTOR_SHARE)
-            apply_gain(c0, n, nc.gpsimd, VECTOR_SHARE)
 
         def quant_h(c0, n):
             nc.vector.quantize_mx(h_codes[:, c0 : c0 + n].bitcast(E4M3X4), h_plane[:, c0 : c0 + n], rounded_h(c0, n))
@@ -209,10 +203,10 @@ def tile_list_camera_error_maps_kernel(tc, xT, wgt, offs, w1, gain, w2_words, w2
         def difference(c0, n, a):
             return xg[a][:, :, c0 : c0 + n]
 
-        def decode(c0, n, a):
+        def decode(c0, n, a, i0=0, count=PACK):
             cols = slice(c0, c0 + n)
             per_bank = HALF // n
-            for j0 in range(0, PACK, per_bank):
+            for j0 in range(i0, i0 + count, per_bank):
                 bank = psum.tile([P, per_bank, n], F32, name="rbank", tag="bank")
                 for u in range(per_bank):
                     g = a * PACK + j0 + u
@@ -279,28 +273,25 @@ def tile_list_camera_error_maps_kernel(tc, xT, wgt, offs, w1, gain, w2_words, w2
         finish(*chunks[0], 0)
         encode(*chunks[3])
         apply_gain(*chunks[2], nc.vector)
-        decode(*chunks[0], 1)
         quant_h(*chunks[2])
-        finish(*chunks[0], 1)
-        share_gain(*chunks[3])
-        for a in range(PASSES):
-            decode(*chunks[1], a)
-            finish(*chunks[1], a)
+        apply_gain(*chunks[3], nc.gpsimd)
+        for k, a in ((0, 1), (1, 0), (1, 1)):
+            decode(*chunks[k], a)
+            finish(*chunks[k], a)
         encode(*chunks[4])
         decode(*chunks[2], 0)
         finish(*chunks[2], 0)
         quant_h(*chunks[3])
-        share_gain(*chunks[4])
-        decode(*chunks[2], 1)
-        finish(*chunks[2], 1)
-        decode(*chunks[3], 0)
-        finish(*chunks[3], 0)
-        quant_h(*chunks[4])
-        for k, a in ((3, 1), (4, 0)):
+        apply_gain(*chunks[4], nc.gpsimd)
+        for k, a in ((2, 1), (3, 0)):
             decode(*chunks[k], a)
-            finish(*chunks[k], a, 0, 2)
-            finish(*chunks[k], a, 2, 2)
-        decode(*chunks[4], 1)
-        finish(*chunks[4], 1, 0, 2)
+            finish(*chunks[k], a)
+        decode(*chunks[3], 1, 0, 2)
+        finish(*chunks[3], 1, 0, 2)
+        quant_h(*chunks[4])
+        for k, a, i0 in ((3, 1, 2), (4, 0, 0), (4, 0, 2), (4, 1, 0)):
+            decode(*chunks[k], a, i0, 2)
+            finish(*chunks[k], a, i0, 2)
+        decode(*chunks[4], 1, 2, 2)
         finish(*chunks[4], 1, 2, 1)
         finish(*chunks[4], 1, 3, 1)

@@ -20,11 +20,13 @@ ALU = mybir.AluOpType
 P = 128
 PACK = 4
 PASSES = 2
-HALF = 512
-QUARTER = 256
-N1 = 128
+BANK = 512
+HALF = S // 2
+QUARTER = S // 4
+N1 = BANK // PACK
 CAMERAS = 8
 GROUP = 16
+W1_LATE = 192
 
 
 def tile_list_camera_error_maps_kernel(tc, xT, wgt, offs, w1, gain, w2_words, w2_scales, prec, out):
@@ -32,85 +34,90 @@ def tile_list_camera_error_maps_kernel(tc, xT, wgt, offs, w1, gain, w2_words, w2
     x_planes = xT.rearrange("(a p i) t -> a i p t", a=PASSES, i=PACK)
     out_rows = out.rearrange("(a p i) j -> a p i j", a=PASSES, i=PACK)
     w1_rows = w1.rearrange("(a p i) r -> a p i r", a=PASSES, i=PACK)
+    chunks = [(0, N1), (N1, N1), (QUARTER, QUARTER), (2 * QUARTER, QUARTER), (3 * QUARTER, QUARTER)]
 
     with ExitStack() as ctx:
         keep = ctx.enter_context(tc.tile_pool(name="keep", bufs=1))
         psum = ctx.enter_context(tc.psum_pool(name="psum", bufs=8))
 
+        def tile(name, shape, dtype, tag=None):
+            return keep.tile(shape, dtype, name=name, tag=tag or name, align_bytes=64)
+
         offsets = keep.tile([P, S // 16], U16, name="offsets")
-        w2_raw = keep.tile([P, 2 * K], U8, name="w2_raw", align_bytes=64)
-        s2_raw = keep.tile([P, K], U8, name="s2_raw", align_bytes=64)
-        w2_codes = keep.tile([P, 2 * K], U8, name="w2_codes", align_bytes=64)
-        w2_plane = keep.tile([P, K], U8, name="w2_plane", align_bytes=64)
-        wgt_sb = keep.tile([P, S], F32, name="wgt_sb")
-        wgt_rows = keep.tile([P, P], F32, name="wgt_rows")
-        wgt_spread = keep.tile([P, S], F32, name="wgt_spread")
-        identity = keep.tile([P, P], F32, name="identity")
-        x_sb = [[keep.tile([P, T], F32, name="x%d%d" % (a, i), align_bytes=64) for i in range(PACK)] for a in range(PASSES)]
-        w1_parts = [(0, 0, H // 2), (0, H // 2, H // 2), (1, 0, H - N1), (1, H - N1, N1)]
-        gain_sb = keep.tile([P, PACK], F32, name="gain_sb")
-        prec_sb = keep.tile([P, PASSES, PACK], F32, name="prec_sb")
+        wgt_rows = tile("wgt_rows", [P, P], F32)
+        wgt_spread = tile("wgt_spread", [P, S], F32)
+        wgt_sb = tile("wgt_sb", [P, S], F32)
+        wgt_first = tile("wgt_first", [P, N1], F32)
+        identity = tile("identity", [P, P], F32)
+        x_sb = [[tile("x%d%d" % (a, i), [P, T], F32) for i in range(PACK)] for a in range(PASSES)]
+        w1_parts = [(0, 0, H // 2), (0, H // 2, H // 2), (1, 0, H - W1_LATE), (1, H - W1_LATE, W1_LATE)]
+        w1_raw = [tile("w1raw%d" % k, [P, PACK, n], F32) for k, (a, r0, n) in enumerate(w1_parts)]
+        w2_raw = tile("w2_raw", [P, 2 * K], U8)
+        s2_raw = tile("s2_raw", [P, K], U8)
+        gain_sb = tile("gain_sb", [P, PACK], F32)
+        prec_sb = tile("prec_sb", [P, PASSES, PACK], F32)
+        xg = [tile("xg%d" % a, [P, PACK, S], F32) for a in range(PASSES)]
+        xb = [tile("xb0", [P, S * PACK], BF16), tile("xb1", [P, S * PACK], BF16, "w1raw1")]
+        x_codes = [tile("xc0", [P, S], U32, "x11"), tile("xc1", [P, S], U32)]
+        x_plane = [tile("xs0", [P, HALF], U8), tile("xs1", [P, S], U8)]
+        late_plane = tile("xs0late", [P, HALF], U8, "wgt_first")
+        w1b = [tile("w1b0", [P, H * PACK], BF16, "x03"), tile("w1b1", [P, H * PACK], BF16)]
+        w1_codes = [tile("w1c%d" % a, [P, H], U32) for a in range(PASSES)]
+        w1_plane = [tile("w1s%d" % a, [P, H], U8) for a in range(PASSES)]
+        w2_codes = tile("w2_codes", [P, 2 * K], U8, "w1b1")
+        w2_plane = tile("w2_plane", [P, K], U8, "w1raw3")
+        th = tile("th", [P, S * PACK], F32)
+        hb = tile("hb", [P, HALF * PACK], BF16)
+        h_codes = tile("hc", [P, S], U32)
+        h_plane = tile("hs", [P, S], U8)
 
-        xg = [keep.tile([P, PACK, S], F32, name="xg%d" % a, align_bytes=64) for a in range(PASSES)]
-        w1_raw = [keep.tile([P, PACK, n], F32, name="w1raw%d" % k, align_bytes=64)[:] for k, (a, r0, n) in enumerate(w1_parts[:-1])]
-        w1_raw.append(xg[1][:, PACK - 1, HALF:S].rearrange("p (i r) -> p i r", i=PACK))
-        xb = [keep.tile([P, S * PACK], BF16, name="xb0", align_bytes=64), keep.tile([P, (S - QUARTER) * PACK], BF16, name="xb1", tag="w1raw2", align_bytes=64)]
-        x_codes = [keep.tile([P, S], U32, name="xc0", tag="x11", align_bytes=64), keep.tile([P, S], U32, name="xc1", align_bytes=64)]
-        x_plane = [keep.tile([P, S], U8, name="xs%d" % a, align_bytes=64) for a in range(PASSES)]
-        w1b = [keep.tile([P, H * PACK], BF16, name="w1b%d" % a, align_bytes=64) for a in range(PASSES)]
-        w1_codes = [keep.tile([P, H], U32, name="w1c%d" % a, align_bytes=64) for a in range(PASSES)]
-        w1_plane = [keep.tile([P, H], U8, name="w1s%d" % a, align_bytes=64) for a in range(PASSES)]
-        th = keep.tile([P, S * PACK], F32, name="th")
-        hb = keep.tile([P, HALF * PACK], BF16, name="hb", align_bytes=64)
-        h_codes = keep.tile([P, S], U32, name="hc", align_bytes=64)
-        h_plane = keep.tile([P, S], U8, name="hs", align_bytes=64)
-
-        nc.vector.memset(wgt_rows[P // 2 : P, :], 0.0)
-        make_identity(nc, identity[:])
-        nc.vector.memset(s2_raw[:].bitcast(U32), 0)
         def load_x(a, i):
             nc.sync.dma_start(x_sb[a][i][:], x_planes[a, i])
 
         def load_w1(k):
             a, r0, n = w1_parts[k]
-            nc.sync.dma_start(w1_raw[k], w1_rows[a][:, :, r0 : r0 + n])
+            nc.sync.dma_start(w1_raw[k][:], w1_rows[a][:, :, r0 : r0 + n])
 
+        nc.vector.memset(wgt_rows[P // 2 : P, :], 0.0)
+        nc.vector.memset(s2_raw[:].bitcast(U32), 0)
+        make_identity(nc, identity[:])
         nc.sync.dma_start(wgt_rows[0 : P // 2, :], wgt.rearrange("(g r) (c e) -> r g c e", r=GROUP, e=P)[0])
         nc.sync.dma_start(offsets[:], offs)
-        nc.sync.dma_start(w2_raw[:].bitcast(I32), w2_words[0].bitcast(I32))
-        scale_rows = w2_scales[0].bitcast(I32).rearrange("(q r) c -> r q c", r=4)
-        for r in range(4):
-            nc.sync.dma_start(s2_raw[r:P:32, :].bitcast(I32), scale_rows[r])
-        load_x(0, 0)
-        load_x(0, 1)
-        load_x(0, 2)
-        load_x(0, 3)
+        for i in range(PACK):
+            load_x(0, i)
         load_x(1, 0)
         load_x(1, 1)
         load_w1(0)
         load_w1(1)
-        load_w1(2)
-        load_w1(3)
         load_x(1, 2)
+        load_w1(2)
         load_x(1, 3)
+        load_w1(3)
+        nc.sync.dma_start(w2_raw[:].bitcast(I32), w2_words[0].bitcast(I32))
+        scale_rows = w2_scales[0].bitcast(I32).rearrange("(q r) c -> r q c", r=4)
+        for r in range(4):
+            nc.sync.dma_start(s2_raw[r:P:32, :].bitcast(I32), scale_rows[r])
         nc.sync.dma_start(gain_sb[:], gain.rearrange("(p t) -> p t", t=PACK))
         nc.sync.dma_start(prec_sb[:], prec.rearrange("(a p i) -> p a i", a=PASSES, i=PACK))
 
-        def spread_wgt():
+        per_bank = BANK // P
+        for h, copy in enumerate((nc.vector.tensor_copy, nc.scalar.copy)):
             turned = psum.tile([P, P], F32, name="turned", tag="bank")
             nc.tensor.transpose(turned[:], wgt_rows[:], identity[:])
-            per_bank = HALF // P
-            for h in range(2):
-                nc.scalar.copy(
-                    wgt_spread[:, h * HALF : (h + 1) * HALF].rearrange("p (c g r) -> p c g r", g=CAMERAS, r=GROUP),
-                    turned[:, 0 : P // 2].rearrange("p (g c) -> p c g", g=CAMERAS)[:, h * per_bank : (h + 1) * per_bank, :].unsqueeze(3).to_broadcast([P, per_bank, CAMERAS, GROUP]),
-                )
-            for h in range(2):
-                back = psum.tile([P, HALF], F32, name="back", tag="bank")
-                for c in range(per_bank):
-                    first = h * HALF + c * P
-                    nc.tensor.transpose(back[:, c * P : (c + 1) * P], wgt_spread[:, first : first + P], identity[:])
-                nc.scalar.copy(wgt_sb[:, h * HALF : (h + 1) * HALF], back[:])
+            copy(
+                wgt_spread[:, h * HALF : (h + 1) * HALF].rearrange("p (c g r) -> p c g r", g=CAMERAS, r=GROUP),
+                turned[:, 0 : P // 2].rearrange("p (g c) -> p c g", g=CAMERAS)[:, h * per_bank : (h + 1) * per_bank, :].unsqueeze(3).to_broadcast([P, per_bank, CAMERAS, GROUP]),
+            )
+        for h, copy in enumerate((nc.vector.tensor_copy, nc.scalar.copy)):
+            back = psum.tile([P, BANK], F32, name="back", tag="bank")
+            for c in range(per_bank):
+                first = h * HALF + c * P
+                nc.tensor.transpose(back[:, c * P : (c + 1) * P], wgt_spread[:, first : first + P], identity[:])
+            copy(wgt_sb[:, h * HALF : (h + 1) * HALF], back[:])
+
+        nc.scalar.copy(wgt_first[:], wgt_sb[:, 0:N1])
+
+        banks = [psum.tile([P, PACK, N1], F32, name="hbank%d" % b, tag="bank") for b in range(S // N1)]
 
         def deal_w2_words():
             nc.vector.tensor_copy(
@@ -124,45 +131,33 @@ def tile_list_camera_error_maps_kernel(tc, xT, wgt, offs, w1, gain, w2_words, w2
                 s2_raw[:].rearrange("p (a q i) -> p a i q", a=PASSES, i=PACK),
             )
 
-        chunks = [(0, N1), (N1, N1), (QUARTER, QUARTER), (2 * QUARTER, QUARTER), (3 * QUARTER, QUARTER)]
-
-        def gather(a, i, c0, n):
+        def gather(a, i, c0, n, weights=wgt_sb):
             window = x_sb[a][i][:].indirect(offsets[:, c0 // 16 : (c0 + n) // 16])
-            nc.vector.tensor_tensor(xg[a][:, i, c0 : c0 + n], window, wgt_sb[:, c0 : c0 + n], ALU.mult)
+            nc.vector.tensor_tensor(xg[a][:, i, c0 : c0 + n], window, weights[:, c0 : c0 + n], ALU.mult)
 
-        def woven(a, c0, n):
-            if a == 0:
-                return xb[0][:, c0 * PACK : (c0 + n) * PACK]
-            if c0 < QUARTER:
-                return xg[1][:, PACK - 1, HALF + 2 * c0 : HALF + 2 * (c0 + n)].bitcast(BF16)
-            return xb[1][:, (c0 - QUARTER) * PACK : (c0 - QUARTER + n) * PACK]
-
-        def weave_pair(a, i0, c0, n, copy):
-            copy(
-                woven(a, c0, n).rearrange("p (c i) -> p c i", i=PACK)[:, :, i0 : i0 + 2],
+        def weave_pair(a, i0, c0, n):
+            nc.scalar.copy(
+                xb[a][:].rearrange("p (c i) -> p c i", i=PACK)[:, c0 : c0 + n, i0 : i0 + 2],
                 xg[a][:, i0 : i0 + 2, c0 : c0 + n].rearrange("p i c -> p c i"),
             )
 
-        def codes_x(a, c0, n):
-            return x_codes[a][:, c0 : c0 + n].bitcast(E4M3X4)
+        def plane_x(a, c0, n):
+            if a == 0 and c0 >= HALF:
+                return late_plane[:, c0 - HALF : c0 - HALF + n]
+            return x_plane[a][:, c0 : c0 + n]
 
         def quant_x(a, c0, n):
-            nc.vector.quantize_mx(
-                codes_x(a, c0, n),
-                x_plane[a][:, c0 : c0 + n],
-                woven(a, c0, n),
-            )
+            nc.vector.quantize_mx(x_codes[a][:, c0 : c0 + n].bitcast(E4M3X4), plane_x(a, c0, n), xb[a][:, c0 * PACK : (c0 + n) * PACK])
 
-        def cast_w1(k, copy=nc.scalar.copy):
+        def cast_w1(k):
             a, r0, n = w1_parts[k]
-            copy(
+            nc.scalar.copy(
                 w1b[a][:].rearrange("p (t m i) -> p m i t", t=PACK, i=PACK)[:, r0 // PACK : (r0 + n) // PACK, :, :],
-                w1_raw[k].rearrange("p i (m t) -> p m i t", t=PACK),
+                w1_raw[k][:].rearrange("p i (m t) -> p m i t", t=PACK),
             )
 
         def quant_w1(a):
-            nc.vector.quantize_mx(w1_codes[a][:, 0:H].bitcast(E4M3X4), w1_plane[a][:], w1b[a][:])
-
+            nc.vector.quantize_mx(w1_codes[a][:].bitcast(E4M3X4), w1_plane[a][:], w1b[a][:])
 
         def encode_pass(b, a):
             for t in range(PACK):
@@ -170,8 +165,8 @@ def tile_list_camera_error_maps_kernel(tc, xT, wgt, offs, w1, gain, w2_words, w2
                     banks[b][:, t, :],
                     lhsT=w1_codes[a][:, t * P : (t + 1) * P].bitcast(E4M3X4),
                     lhsT_scale=w1_plane[a][:, t * P : (t + 1) * P],
-                    rhs=codes_x(a, b * N1, N1),
-                    rhs_scale=x_plane[a][:, b * N1 : (b + 1) * N1],
+                    rhs=x_codes[a][:, b * N1 : (b + 1) * N1].bitcast(E4M3X4),
+                    rhs_scale=plane_x(a, b * N1, N1),
                     start=(a == 0 and t == 0),
                     stop=(a == PASSES - 1 and t == PACK - 1),
                 )
@@ -180,7 +175,7 @@ def tile_list_camera_error_maps_kernel(tc, xT, wgt, offs, w1, gain, w2_words, w2
             for b in range(c0 // N1, (c0 + n) // N1):
                 encode_pass(b, 1)
                 nc.scalar.activation(
-                    th[:, b * N1 * PACK : (b + 1) * N1 * PACK].rearrange("p (n t) -> p n t", t=PACK),
+                    th[:, b * BANK : (b + 1) * BANK].rearrange("p (n t) -> p n t", t=PACK),
                     banks[b][:].rearrange("p t n -> p n t"),
                     ACT.Tanh,
                 )
@@ -200,98 +195,88 @@ def tile_list_camera_error_maps_kernel(tc, xT, wgt, offs, w1, gain, w2_words, w2
         def quant_h(c0, n):
             nc.vector.quantize_mx(h_codes[:, c0 : c0 + n].bitcast(E4M3X4), h_plane[:, c0 : c0 + n], rounded_h(c0, n))
 
-        def difference(c0, n, a):
-            return xg[a][:, :, c0 : c0 + n]
-
-        def decode(c0, n, a, i0=0, count=PACK):
+        def errors(k, a, i0, count, queue=nc.sync):
+            c0, n = chunks[k]
             cols = slice(c0, c0 + n)
-            per_bank = HALF // n
-            for j0 in range(i0, i0 + count, per_bank):
-                bank = psum.tile([P, per_bank, n], F32, name="rbank", tag="bank")
-                for u in range(per_bank):
-                    g = a * PACK + j0 + u
-                    nc.tensor.matmul_mx(
-                        bank[:, u, :],
-                        lhsT=w2_codes[:, g * 2 * P : (g + 1) * 2 * P].bitcast(E2M1X4),
-                        lhsT_scale=w2_plane[:, g * P : (g + 1) * P],
-                        rhs=h_codes[:, cols].bitcast(E4M3X4),
-                        rhs_scale=h_plane[:, cols],
-                        start=True,
-                        stop=True,
-                    )
-                nc.vector.tensor_tensor(difference(c0, n, a)[:, j0 : j0 + per_bank, :], bank[:], xg[a][:, j0 : j0 + per_bank, cols], ALU.subtract)
-
-        def finish(c0, n, a, i0=0, count=PACK):
-            cols = slice(c0, c0 + n)
+            bank = psum.tile([P, count, n], F32, name="rbank", tag="bank")
+            for u in range(count):
+                g = a * PACK + i0 + u
+                nc.tensor.matmul_mx(
+                    bank[:, u, :],
+                    lhsT=w2_codes[:, g * 2 * P : (g + 1) * 2 * P].bitcast(E2M1X4),
+                    lhsT_scale=w2_plane[:, g * P : (g + 1) * P],
+                    rhs=h_codes[:, cols].bitcast(E4M3X4),
+                    rhs_scale=h_plane[:, cols],
+                    start=True,
+                    stop=True,
+                )
+            rows = xg[a][:, i0 : i0 + count, cols]
+            nc.vector.tensor_tensor(rows, bank[:], rows, ALU.subtract)
             for i in range(i0, i0 + count):
-                nc.scalar.activation(xg[a][:, i, cols], difference(c0, n, a)[:, i, :], ACT.Square, scale=prec_sb[:, a, i : i + 1])
-            nc.sync.dma_start(out_rows[a][:, i0 : i0 + count, cols], xg[a][:, i0 : i0 + count, cols])
+                nc.scalar.activation(xg[a][:, i, cols], xg[a][:, i, cols], ACT.Square, scale=prec_sb[:, a, i : i + 1])
+            queue.dma_start(out_rows[a][:, i0 : i0 + count, cols], rows)
 
-        spread_wgt()
-        banks = [psum.tile([P, PACK, N1], F32, name="hbank%d" % b, tag="bank") for b in range(S // N1)]
-        deal_w2_words()
-        deal_w2_scales()
         for h in range(2):
             gather(0, 0, h * HALF, HALF)
         gather(0, 1, 0, S)
-        weave_pair(0, 0, 0, S, nc.scalar.copy)
+        weave_pair(0, 0, 0, S)
         gather(0, 2, 0, S)
         for h in range(2):
             gather(0, 3, h * HALF, HALF)
-            weave_pair(0, 2, h * HALF, HALF, nc.scalar.copy)
+            weave_pair(0, 2, h * HALF, HALF)
         cast_w1(0)
         cast_w1(1)
-        for i in range(2):
-            gather(1, i, 0, S)
-        quant_x(0, 0, S)
+        gather(1, 0, 0, S)
+        gather(1, 1, 0, S)
+        quant_x(0, 0, HALF)
         quant_w1(0)
-        cast_w1(2)
-        cast_w1(3, nc.vector.tensor_copy)
-        weave_pair(1, 0, 0, QUARTER, nc.scalar.copy)
-        weave_pair(1, 0, QUARTER, S - QUARTER, nc.scalar.copy)
-        for b in range(S // N1):
+        weave_pair(1, 0, 0, S)
+        for b in range(HALF // N1):
             encode_pass(b, 0)
-        quant_w1(1)
         gather(1, 2, 0, S)
-        for k in range(3):
-            gather(1, 3, *chunks[k])
-            weave_pair(1, 2, *chunks[k], nc.scalar.copy)
-        for k in range(2):
-            quant_x(1, *chunks[k])
-            encode(*chunks[k])
-            gather(1, 3, *chunks[k + 3])
-        weave_pair(1, 2, *chunks[3], nc.scalar.copy)
+        cast_w1(2)
+        gather(1, 3, 0, N1, wgt_first)
+        quant_x(0, HALF, HALF)
+        for b in range(HALF // N1, S // N1):
+            encode_pass(b, 0)
+        for c0, n in ((N1, N1), (QUARTER, QUARTER), (HALF, HALF)):
+            gather(1, 3, c0, n)
+        weave_pair(1, 2, *chunks[0])
+        cast_w1(3)
+        weave_pair(1, 2, *chunks[1])
+        quant_x(1, 0, QUARTER)
+        quant_w1(1)
+        deal_w2_words()
+        weave_pair(1, 2, *chunks[2])
+        encode(*chunks[0])
+        weave_pair(1, 2, *chunks[3])
         quant_x(1, *chunks[2])
+        deal_w2_scales()
+        encode(*chunks[1])
         apply_gain(*chunks[0], nc.vector)
-        weave_pair(1, 2, *chunks[4], nc.scalar.copy)
+        weave_pair(1, 2, *chunks[4])
         encode(*chunks[2])
         apply_gain(*chunks[1], nc.vector)
         quant_h(*chunks[0])
         quant_x(1, HALF, HALF)
         quant_h(*chunks[1])
-        decode(*chunks[0], 0)
-        finish(*chunks[0], 0)
+        errors(0, 0, 0, PACK)
         encode(*chunks[3])
         apply_gain(*chunks[2], nc.vector)
         quant_h(*chunks[2])
         apply_gain(*chunks[3], nc.gpsimd)
-        for k, a in ((0, 1), (1, 0), (1, 1)):
-            decode(*chunks[k], a)
-            finish(*chunks[k], a)
+        errors(0, 1, 0, PACK)
+        errors(1, 0, 0, PACK)
+        errors(1, 1, 0, PACK)
         encode(*chunks[4])
-        decode(*chunks[2], 0)
-        finish(*chunks[2], 0)
+        for i0 in (0, 2):
+            errors(2, 0, i0, 2)
         quant_h(*chunks[3])
         apply_gain(*chunks[4], nc.gpsimd)
-        for k, a in ((2, 1), (3, 0)):
-            decode(*chunks[k], a)
-            finish(*chunks[k], a)
-        decode(*chunks[3], 1, 0, 2)
-        finish(*chunks[3], 1, 0, 2)
+        for k, a, i0 in ((2, 1, 0), (2, 1, 2), (3, 0, 0), (3, 0, 2), (3, 1, 0)):
+            errors(k, a, i0, 2)
         quant_h(*chunks[4])
         for k, a, i0 in ((3, 1, 2), (4, 0, 0), (4, 0, 2), (4, 1, 0)):
-            decode(*chunks[k], a, i0, 2)
-            finish(*chunks[k], a, i0, 2)
-        decode(*chunks[4], 1, 2, 2)
-        finish(*chunks[4], 1, 2, 1)
-        finish(*chunks[4], 1, 3, 1)
+            errors(k, a, i0, 2)
+        errors(4, 1, 2, 1)
+        errors(4, 1, 3, 1, nc.scalar)

@@ -26,7 +26,7 @@ QUARTER = S // 4
 N1 = BANK // PACK
 CAMERAS = 8
 GROUP = 16
-W1_LATE = 192
+W1_LATE = 256
 
 
 def tile_list_camera_error_maps_kernel(tc, xT, wgt, offs, w1, gain, w2_words, w2_scales, prec, out):
@@ -195,7 +195,7 @@ def tile_list_camera_error_maps_kernel(tc, xT, wgt, offs, w1, gain, w2_words, w2
         def quant_h(c0, n):
             nc.vector.quantize_mx(h_codes[:, c0 : c0 + n].bitcast(E4M3X4), h_plane[:, c0 : c0 + n], rounded_h(c0, n))
 
-        def errors(k, a, i0, count, queue=nc.sync):
+        def errors(k, a, i0, count):
             c0, n = chunks[k]
             cols = slice(c0, c0 + n)
             bank = psum.tile([P, count, n], F32, name="rbank", tag="bank")
@@ -214,7 +214,14 @@ def tile_list_camera_error_maps_kernel(tc, xT, wgt, offs, w1, gain, w2_words, w2
             nc.vector.tensor_tensor(rows, bank[:], rows, ALU.subtract)
             for i in range(i0, i0 + count):
                 nc.scalar.activation(xg[a][:, i, cols], xg[a][:, i, cols], ACT.Square, scale=prec_sb[:, a, i : i + 1])
-            queue.dma_start(out_rows[a][:, i0 : i0 + count, cols], rows)
+
+        def store(c0, n, a, i0, count, queue=nc.sync):
+            queue.dma_start(out_rows[a][:, i0 : i0 + count, c0 : c0 + n], xg[a][:, i0 : i0 + count, c0 : c0 + n])
+
+        def errors_pass(k, a):
+            for i0 in (0, 2):
+                errors(k, a, i0, 2)
+            store(*chunks[k], a, 0, PACK)
 
         for h in range(2):
             gather(0, 0, h * HALF, HALF)
@@ -261,22 +268,33 @@ def tile_list_camera_error_maps_kernel(tc, xT, wgt, offs, w1, gain, w2_words, w2
         quant_x(1, HALF, HALF)
         quant_h(*chunks[1])
         errors(0, 0, 0, PACK)
+        store(*chunks[0], 0, 0, PACK)
         encode(*chunks[3])
         apply_gain(*chunks[2], nc.vector)
         quant_h(*chunks[2])
         apply_gain(*chunks[3], nc.gpsimd)
-        errors(0, 1, 0, PACK)
         errors(1, 0, 0, PACK)
+        store(*chunks[1], 0, 0, PACK)
+        errors(0, 1, 0, PACK)
         errors(1, 1, 0, PACK)
+        store(0, QUARTER, 1, 0, PACK)
         encode(*chunks[4])
-        for i0 in (0, 2):
-            errors(2, 0, i0, 2)
+        errors_pass(2, 0)
         quant_h(*chunks[3])
         apply_gain(*chunks[4], nc.gpsimd)
-        for k, a, i0 in ((2, 1, 0), (2, 1, 2), (3, 0, 0), (3, 0, 2), (3, 1, 0)):
-            errors(k, a, i0, 2)
+        errors_pass(2, 1)
+        errors_pass(3, 0)
+        errors(3, 1, 0, 2)
+        store(*chunks[3], 1, 0, 2)
         quant_h(*chunks[4])
-        for k, a, i0 in ((3, 1, 2), (4, 0, 0), (4, 0, 2), (4, 1, 0)):
-            errors(k, a, i0, 2)
+        errors(3, 1, 2, 2)
+        store(*chunks[3], 1, 2, 2)
+        for i0 in (0, 2):
+            errors(4, 0, i0, 2)
+            store(*chunks[4], 0, i0, 2)
+        errors(4, 1, 0, 2)
+        store(*chunks[4], 1, 0, 2)
         errors(4, 1, 2, 1)
-        errors(4, 1, 3, 1, nc.scalar)
+        store(*chunks[4], 1, 2, 1)
+        errors(4, 1, 3, 1)
+        store(*chunks[4], 1, 3, 1, nc.scalar)

@@ -26,7 +26,6 @@ QUARTER = S // 4
 N1 = BANK // PACK
 CAMERAS = 8
 GROUP = 16
-W1_LATE = 256
 
 
 def tile_list_camera_error_maps_kernel(tc, xT, wgt, offs, w1, gain, w2_words, w2_scales, prec, out):
@@ -38,6 +37,7 @@ def tile_list_camera_error_maps_kernel(tc, xT, wgt, offs, w1, gain, w2_words, w2
 
     with ExitStack() as ctx:
         keep = ctx.enter_context(tc.tile_pool(name="keep", bufs=1))
+        laid = ctx.enter_context(tc.tile_pool(name="laid", bufs=1))
         psum = ctx.enter_context(tc.psum_pool(name="psum", bufs=8))
 
         def tile(name, shape, dtype, tag=None):
@@ -47,25 +47,29 @@ def tile_list_camera_error_maps_kernel(tc, xT, wgt, offs, w1, gain, w2_words, w2
         wgt_rows = tile("wgt_rows", [P, P], F32)
         wgt_spread = tile("wgt_spread", [P, S], F32)
         wgt_sb = tile("wgt_sb", [P, S], F32)
-        wgt_first = tile("wgt_first", [P, N1], F32)
         identity = tile("identity", [P, P], F32)
         x_sb = [[tile("x%d%d" % (a, i), [P, T], F32) for i in range(PACK)] for a in range(PASSES)]
-        w1_parts = [(0, 0, H // 2), (0, H // 2, H // 2), (1, 0, H - W1_LATE), (1, H - W1_LATE, W1_LATE)]
-        w1_raw = [tile("w1raw%d" % k, [P, PACK, n], F32) for k, (a, r0, n) in enumerate(w1_parts)]
+        w1_raw = [tile("w1raw%d" % k, [P, PACK, H // 2], F32) for k in range(2 * PASSES)]
         w2_raw = tile("w2_raw", [P, 2 * K], U8)
         s2_raw = tile("s2_raw", [P, K], U8)
         gain_sb = tile("gain_sb", [P, PACK], F32)
         prec_sb = tile("prec_sb", [P, PASSES, PACK], F32)
         xg = [tile("xg%d" % a, [P, PACK, S], F32) for a in range(PASSES)]
-        xb = [tile("xb0", [P, S * PACK], BF16), tile("xb1", [P, S * PACK], BF16, "w1raw1")]
-        x_codes = [tile("xc0", [P, S], U32, "x11"), tile("xc1", [P, S], U32)]
-        x_plane = [tile("xs0", [P, HALF], U8), tile("xs1", [P, S], U8)]
-        late_plane = tile("xs0late", [P, HALF], U8, "wgt_first")
-        w1b = [tile("w1b0", [P, H * PACK], BF16, "x03"), tile("w1b1", [P, H * PACK], BF16)]
+        xb0 = tile("xb0", [P, S * PACK], BF16)
+        xb1 = [tile("xb1_front", [P, QUARTER * PACK], BF16, "w1raw0"), tile("xb1_back", [P, 3 * QUARTER * PACK], BF16, "w1raw2")]
+        x0_codes = tile("xc0", [P, S], U32, "x11")
+        x_plane = [tile("xs%d" % a, [P, S], U8) for a in range(PASSES)]
+        w1b = [tile("w1b0", [P, H * PACK], BF16), laid.tile([P, H * PACK], BF16, name="w1b1", offset=0, align_bytes=64)]
+        x1_codes = [
+            tile("xc10", [P, QUARTER], U32, "w1raw3"),
+            laid.tile([P, QUARTER], U32, name="xc11", offset=3 * K, align_bytes=64),
+            tile("xc12", [P, QUARTER], U32),
+            tile("xc13", [P, QUARTER], U32),
+        ]
         w1_codes = [tile("w1c%d" % a, [P, H], U32) for a in range(PASSES)]
         w1_plane = [tile("w1s%d" % a, [P, H], U8) for a in range(PASSES)]
-        w2_codes = tile("w2_codes", [P, 2 * K], U8, "w1b1")
-        w2_plane = tile("w2_plane", [P, K], U8, "w1raw3")
+        w2_codes = laid.tile([P, 2 * K], U8, name="w2_codes", offset=0, align_bytes=64)
+        w2_plane = laid.tile([P, K], U8, name="w2_plane", offset=2 * K, align_bytes=64)
         th = tile("th", [P, S * PACK], F32)
         hb = tile("hb", [P, HALF * PACK], BF16)
         h_codes = tile("hc", [P, S], U32)
@@ -75,8 +79,8 @@ def tile_list_camera_error_maps_kernel(tc, xT, wgt, offs, w1, gain, w2_words, w2
             nc.sync.dma_start(x_sb[a][i][:], x_planes[a, i])
 
         def load_w1(k):
-            a, r0, n = w1_parts[k]
-            nc.sync.dma_start(w1_raw[k][:], w1_rows[a][:, :, r0 : r0 + n])
+            r0 = k % 2 * (H // 2)
+            nc.sync.dma_start(w1_raw[k][:], w1_rows[k // 2][:, :, r0 : r0 + H // 2])
 
         nc.vector.memset(wgt_rows[P // 2 : P, :], 0.0)
         nc.vector.memset(s2_raw[:].bitcast(U32), 0)
@@ -88,34 +92,32 @@ def tile_list_camera_error_maps_kernel(tc, xT, wgt, offs, w1, gain, w2_words, w2
         load_x(1, 0)
         load_x(1, 1)
         load_w1(0)
-        load_w1(1)
         load_x(1, 2)
-        load_w1(2)
+        load_w1(1)
         load_x(1, 3)
+        load_w1(2)
         load_w1(3)
         nc.sync.dma_start(w2_raw[:].bitcast(I32), w2_words[0].bitcast(I32))
         scale_rows = w2_scales[0].bitcast(I32).rearrange("(q r) c -> r q c", r=4)
         for r in range(4):
             nc.sync.dma_start(s2_raw[r:P:32, :].bitcast(I32), scale_rows[r])
-        nc.sync.dma_start(gain_sb[:], gain.rearrange("(p t) -> p t", t=PACK))
-        nc.sync.dma_start(prec_sb[:], prec.rearrange("(a p i) -> p a i", a=PASSES, i=PACK))
+        nc.scalar.dma_start(gain_sb[:], gain.rearrange("(p t) -> p t", t=PACK))
+        nc.scalar.dma_start(prec_sb[:], prec.rearrange("(a p i) -> p a i", a=PASSES, i=PACK))
 
-        per_bank = BANK // P
-        for h, copy in enumerate((nc.vector.tensor_copy, nc.scalar.copy)):
+        spreads = [(0, 2, nc.vector.tensor_copy), (2, 2, nc.scalar.copy), (4, 4, nc.scalar.copy)]
+        for h in range(2):
             turned = psum.tile([P, P], F32, name="turned", tag="bank")
             nc.tensor.transpose(turned[:], wgt_rows[:], identity[:])
-            copy(
-                wgt_spread[:, h * HALF : (h + 1) * HALF].rearrange("p (c g r) -> p c g r", g=CAMERAS, r=GROUP),
-                turned[:, 0 : P // 2].rearrange("p (g c) -> p c g", g=CAMERAS)[:, h * per_bank : (h + 1) * per_bank, :].unsqueeze(3).to_broadcast([P, per_bank, CAMERAS, GROUP]),
-            )
-        for h, copy in enumerate((nc.vector.tensor_copy, nc.scalar.copy)):
-            back = psum.tile([P, BANK], F32, name="back", tag="bank")
-            for c in range(per_bank):
-                first = h * HALF + c * P
-                nc.tensor.transpose(back[:, c * P : (c + 1) * P], wgt_spread[:, first : first + P], identity[:])
-            copy(wgt_sb[:, h * HALF : (h + 1) * HALF], back[:])
-
-        nc.scalar.copy(wgt_first[:], wgt_sb[:, 0:N1])
+            for c0, n, copy in spreads[h : 2 * h + 1]:
+                copy(
+                    wgt_spread[:, c0 * P : (c0 + n) * P].rearrange("p (c g r) -> p c g r", g=CAMERAS, r=GROUP),
+                    turned[:, 0 : P // 2].rearrange("p (g c) -> p c g", g=CAMERAS)[:, c0 : c0 + n, :].unsqueeze(3).to_broadcast([P, n, CAMERAS, GROUP]),
+                )
+        for c0, n, copy in spreads:
+            back = psum.tile([P, n * P], F32, name="back", tag="bank")
+            for c in range(n):
+                nc.tensor.transpose(back[:, c * P : (c + 1) * P], wgt_spread[:, (c0 + c) * P : (c0 + c + 1) * P], identity[:])
+            copy(wgt_sb[:, c0 * P : (c0 + n) * P], back[:])
 
         banks = [psum.tile([P, PACK, N1], F32, name="hbank%d" % b, tag="bank") for b in range(S // N1)]
 
@@ -131,28 +133,41 @@ def tile_list_camera_error_maps_kernel(tc, xT, wgt, offs, w1, gain, w2_words, w2
                 s2_raw[:].rearrange("p (a q i) -> p a i q", a=PASSES, i=PACK),
             )
 
-        def gather(a, i, c0, n, weights=wgt_sb):
+        def gather(a, i, c0, n):
             window = x_sb[a][i][:].indirect(offsets[:, c0 // 16 : (c0 + n) // 16])
-            nc.vector.tensor_tensor(xg[a][:, i, c0 : c0 + n], window, weights[:, c0 : c0 + n], ALU.mult)
+            nc.vector.tensor_tensor(xg[a][:, i, c0 : c0 + n], window, wgt_sb[:, c0 : c0 + n], ALU.mult)
+
+        def rounded_x(a, c0, n):
+            if a == 0:
+                return xb0[:, c0 * PACK : (c0 + n) * PACK]
+            if c0 < QUARTER:
+                return xb1[0][:]
+            return xb1[1][:, (c0 - QUARTER) * PACK : (c0 - QUARTER + n) * PACK]
 
         def weave_pair(a, i0, c0, n):
             nc.scalar.copy(
-                xb[a][:].rearrange("p (c i) -> p c i", i=PACK)[:, c0 : c0 + n, i0 : i0 + 2],
+                rounded_x(a, c0, n).rearrange("p (c i) -> p c i", i=PACK)[:, :, i0 : i0 + 2],
                 xg[a][:, i0 : i0 + 2, c0 : c0 + n].rearrange("p i c -> p c i"),
             )
 
-        def plane_x(a, c0, n):
-            if a == 0 and c0 >= HALF:
-                return late_plane[:, c0 - HALF : c0 - HALF + n]
-            return x_plane[a][:, c0 : c0 + n]
+        def weave_four(a, c0, n):
+            nc.scalar.copy(
+                rounded_x(a, c0, n).rearrange("p (c e i) -> p c i e", e=PACK, i=PACK),
+                xg[a][:, :, c0 : c0 + n].rearrange("p i (c e) -> p c i e", e=PACK),
+            )
+
+        def codes_x(a, c0, n):
+            if a == 0:
+                return x0_codes[:, c0 : c0 + n].bitcast(E4M3X4)
+            return x1_codes[c0 // QUARTER][:, c0 % QUARTER : c0 % QUARTER + n].bitcast(E4M3X4)
 
         def quant_x(a, c0, n):
-            nc.vector.quantize_mx(x_codes[a][:, c0 : c0 + n].bitcast(E4M3X4), plane_x(a, c0, n), xb[a][:, c0 * PACK : (c0 + n) * PACK])
+            nc.vector.quantize_mx(codes_x(a, c0, n), x_plane[a][:, c0 : c0 + n], rounded_x(a, c0, n))
 
-        def cast_w1(k):
-            a, r0, n = w1_parts[k]
-            nc.scalar.copy(
-                w1b[a][:].rearrange("p (t m i) -> p m i t", t=PACK, i=PACK)[:, r0 // PACK : (r0 + n) // PACK, :, :],
+        def cast_w1(k, copy):
+            m0 = k % 2 * (P // 2)
+            copy(
+                w1b[k // 2][:].rearrange("p (t m i) -> p m i t", t=PACK, i=PACK)[:, m0 : m0 + P // 2, :, :],
                 w1_raw[k][:].rearrange("p i (m t) -> p m i t", t=PACK),
             )
 
@@ -165,37 +180,42 @@ def tile_list_camera_error_maps_kernel(tc, xT, wgt, offs, w1, gain, w2_words, w2
                     banks[b][:, t, :],
                     lhsT=w1_codes[a][:, t * P : (t + 1) * P].bitcast(E4M3X4),
                     lhsT_scale=w1_plane[a][:, t * P : (t + 1) * P],
-                    rhs=x_codes[a][:, b * N1 : (b + 1) * N1].bitcast(E4M3X4),
-                    rhs_scale=plane_x(a, b * N1, N1),
+                    rhs=codes_x(a, b * N1, N1),
+                    rhs_scale=x_plane[a][:, b * N1 : (b + 1) * N1],
                     start=(a == 0 and t == 0),
                     stop=(a == PASSES - 1 and t == PACK - 1),
                 )
 
-        def encode(c0, n):
-            for b in range(c0 // N1, (c0 + n) // N1):
-                encode_pass(b, 1)
-                nc.scalar.activation(
-                    th[:, b * BANK : (b + 1) * BANK].rearrange("p (n t) -> p n t", t=PACK),
-                    banks[b][:].rearrange("p t n -> p n t"),
-                    ACT.Tanh,
-                )
+        def close_quarter(q):
+            quant_x(1, q * QUARTER, QUARTER)
+            encode_pass(2 * q, 1)
+            encode_pass(2 * q + 1, 1)
 
-        def rounded_h(c0, n):
-            first = min(c0, QUARTER) * PACK
-            return hb[:, first : first + n * PACK]
+        def tanh(b):
+            nc.scalar.activation(
+                th[:, b * BANK : (b + 1) * BANK].rearrange("p (n t) -> p n t", t=PACK),
+                banks[b][:].rearrange("p t n -> p n t"),
+                ACT.Tanh,
+            )
 
-        def apply_gain(c0, n, engine):
+        def rounded_h(k):
+            first = min(chunks[k][0], QUARTER) * PACK
+            return hb[:, first : first + chunks[k][1] * PACK]
+
+        def apply_gain(k, engine):
+            c0, n = chunks[k]
             engine.tensor_tensor(
-                rounded_h(c0, n).rearrange("p (n t) -> p n t", t=PACK),
+                rounded_h(k).rearrange("p (n t) -> p n t", t=PACK),
                 th[:, c0 * PACK : (c0 + n) * PACK].rearrange("p (n t) -> p n t", t=PACK),
                 gain_sb[:].unsqueeze(1).to_broadcast([P, n, PACK]),
                 ALU.mult,
             )
 
-        def quant_h(c0, n):
-            nc.vector.quantize_mx(h_codes[:, c0 : c0 + n].bitcast(E4M3X4), h_plane[:, c0 : c0 + n], rounded_h(c0, n))
+        def quant_h(k):
+            c0, n = chunks[k]
+            nc.vector.quantize_mx(h_codes[:, c0 : c0 + n].bitcast(E4M3X4), h_plane[:, c0 : c0 + n], rounded_h(k))
 
-        def errors(k, a, i0, count):
+        def subtract(k, a, i0, count):
             c0, n = chunks[k]
             cols = slice(c0, c0 + n)
             bank = psum.tile([P, count, n], F32, name="rbank", tag="bank")
@@ -212,89 +232,91 @@ def tile_list_camera_error_maps_kernel(tc, xT, wgt, offs, w1, gain, w2_words, w2
                 )
             rows = xg[a][:, i0 : i0 + count, cols]
             nc.vector.tensor_tensor(rows, bank[:], rows, ALU.subtract)
+
+        def square(c0, n, a, i0, count):
             for i in range(i0, i0 + count):
-                nc.scalar.activation(xg[a][:, i, cols], xg[a][:, i, cols], ACT.Square, scale=prec_sb[:, a, i : i + 1])
+                nc.scalar.activation(xg[a][:, i, c0 : c0 + n], xg[a][:, i, c0 : c0 + n], ACT.Square, scale=prec_sb[:, a, i : i + 1])
 
         def store(c0, n, a, i0, count, queue=nc.sync):
             queue.dma_start(out_rows[a][:, i0 : i0 + count, c0 : c0 + n], xg[a][:, i0 : i0 + count, c0 : c0 + n])
 
+        def finish(c0, n, a, i0, count, queue=nc.sync):
+            square(c0, n, a, i0, count)
+            store(c0, n, a, i0, count, queue)
+
         def errors_pass(k, a):
             for i0 in (0, 2):
-                errors(k, a, i0, 2)
+                subtract(k, a, i0, 2)
+                square(*chunks[k], a, i0, 2)
             store(*chunks[k], a, 0, PACK)
 
-        for h in range(2):
-            gather(0, 0, h * HALF, HALF)
+        for c0, n, copy in spreads:
+            gather(0, 0, c0 * P, n * P)
         gather(0, 1, 0, S)
         weave_pair(0, 0, 0, S)
         gather(0, 2, 0, S)
-        for h in range(2):
-            gather(0, 3, h * HALF, HALF)
-            weave_pair(0, 2, h * HALF, HALF)
-        cast_w1(0)
-        cast_w1(1)
+        gather(0, 3, 0, S)
+        weave_pair(0, 2, 0, S)
         gather(1, 0, 0, S)
         gather(1, 1, 0, S)
-        quant_x(0, 0, HALF)
-        quant_w1(0)
-        weave_pair(1, 0, 0, S)
-        for b in range(HALF // N1):
-            encode_pass(b, 0)
+        quant_x(0, 0, S)
+        cast_w1(0, nc.scalar.copy)
+        weave_pair(1, 0, 0, QUARTER)
         gather(1, 2, 0, S)
-        cast_w1(2)
-        gather(1, 3, 0, N1, wgt_first)
-        quant_x(0, HALF, HALF)
-        for b in range(HALF // N1, S // N1):
+        cast_w1(1, nc.scalar.copy)
+        quant_w1(0)
+        for b in range(S // N1):
             encode_pass(b, 0)
-        for c0, n in ((N1, N1), (QUARTER, QUARTER), (HALF, HALF)):
-            gather(1, 3, c0, n)
-        weave_pair(1, 2, *chunks[0])
-        cast_w1(3)
-        weave_pair(1, 2, *chunks[1])
+        for q in range(4):
+            gather(1, 3, q * QUARTER, QUARTER)
+        weave_pair(1, 2, 0, QUARTER)
+        cast_w1(2, nc.scalar.copy)
+        cast_w1(3, nc.vector.tensor_copy)
         quant_x(1, 0, QUARTER)
         quant_w1(1)
+        encode_pass(0, 1)
+        encode_pass(1, 1)
+        for q in range(1, 4):
+            weave_four(1, q * QUARTER, QUARTER)
         deal_w2_words()
-        weave_pair(1, 2, *chunks[2])
-        encode(*chunks[0])
-        weave_pair(1, 2, *chunks[3])
-        quant_x(1, *chunks[2])
+        close_quarter(1)
         deal_w2_scales()
-        encode(*chunks[1])
-        apply_gain(*chunks[0], nc.vector)
-        weave_pair(1, 2, *chunks[4])
-        encode(*chunks[2])
-        apply_gain(*chunks[1], nc.vector)
-        quant_h(*chunks[0])
-        quant_x(1, HALF, HALF)
-        quant_h(*chunks[1])
-        errors(0, 0, 0, PACK)
-        store(*chunks[0], 0, 0, PACK)
-        encode(*chunks[3])
-        apply_gain(*chunks[2], nc.vector)
-        quant_h(*chunks[2])
-        apply_gain(*chunks[3], nc.gpsimd)
-        errors(1, 0, 0, PACK)
-        store(*chunks[1], 0, 0, PACK)
-        errors(0, 1, 0, PACK)
-        errors(1, 1, 0, PACK)
-        store(0, QUARTER, 1, 0, PACK)
-        encode(*chunks[4])
+        close_quarter(2)
+        for b in range(6):
+            tanh(b)
+        apply_gain(0, nc.vector)
+        close_quarter(3)
+        quant_h(0)
+        apply_gain(1, nc.vector)
+        apply_gain(2, nc.vector)
+        quant_h(1)
+        subtract(0, 0, 0, PACK)
+        quant_h(2)
+        apply_gain(3, nc.gpsimd)
+        finish(*chunks[0], 0, 0, PACK)
+        subtract(1, 0, 0, PACK)
+        finish(*chunks[1], 0, 0, PACK)
+        subtract(0, 1, 0, PACK)
+        subtract(1, 1, 0, PACK)
+        finish(0, QUARTER, 1, 0, PACK)
+        tanh(6)
+        tanh(7)
         errors_pass(2, 0)
-        quant_h(*chunks[3])
-        apply_gain(*chunks[4], nc.gpsimd)
+        quant_h(3)
+        apply_gain(4, nc.gpsimd)
         errors_pass(2, 1)
         errors_pass(3, 0)
-        errors(3, 1, 0, 2)
-        store(*chunks[3], 1, 0, 2)
-        quant_h(*chunks[4])
-        errors(3, 1, 2, 2)
-        store(*chunks[3], 1, 2, 2)
+        subtract(3, 1, 0, 2)
+        finish(*chunks[3], 1, 0, 2)
+        quant_h(4)
+        subtract(3, 1, 2, 2)
+        finish(*chunks[3], 1, 2, 2)
         for i0 in (0, 2):
-            errors(4, 0, i0, 2)
-            store(*chunks[4], 0, i0, 2)
-        errors(4, 1, 0, 2)
-        store(*chunks[4], 1, 0, 2)
-        errors(4, 1, 2, 1)
-        store(*chunks[4], 1, 2, 1)
-        errors(4, 1, 3, 1)
-        store(*chunks[4], 1, 3, 1, nc.scalar)
+            subtract(4, 0, i0, 2)
+            finish(*chunks[4], 0, i0, 2)
+        subtract(4, 1, 0, 2)
+        finish(*chunks[4], 1, 0, 2)
+        subtract(4, 1, 2, 1)
+        finish(*chunks[4], 1, 2, 1)
+        subtract(4, 1, 3, 1)
+        finish(*chunks[4], 1, 3, 1, nc.scalar)

@@ -56,7 +56,7 @@ def tile_list_camera_error_maps_kernel(tc, xT, wgt, offs, w1, gain, w2_words, w2
         prec_sb = tile("prec_sb", [P, PASSES, PACK], F32)
         xg = [tile("xg%d" % a, [P, PACK, S], F32) for a in range(PASSES)]
         xb0 = tile("xb0", [P, S * PACK], BF16)
-        xb1 = [tile("xb1_front", [P, QUARTER * PACK], BF16, "w1raw0"), tile("xb1_back", [P, 3 * QUARTER * PACK], BF16, "w1raw2")]
+        xb1 = [tile("xb1_front", [P, QUARTER * PACK], BF16, "w1raw0"), tile("xb1_back", [P, HALF * PACK], BF16, "w1raw2")]
         x0_codes = tile("xc0", [P, S], U32, "x11")
         x_plane = [tile("xs%d" % a, [P, S], U8) for a in range(PASSES)]
         w1b = [tile("w1b0", [P, H * PACK], BF16), laid.tile([P, H * PACK], BF16, name="w1b1", offset=0, align_bytes=64)]
@@ -70,7 +70,8 @@ def tile_list_camera_error_maps_kernel(tc, xT, wgt, offs, w1, gain, w2_words, w2
         w1_plane = [tile("w1s%d" % a, [P, H], U8) for a in range(PASSES)]
         w2_codes = laid.tile([P, 2 * K], U8, name="w2_codes", offset=0, align_bytes=64)
         w2_plane = laid.tile([P, K], U8, name="w2_plane", offset=2 * K, align_bytes=64)
-        th = tile("th", [P, S * PACK], F32)
+        th = [tile("th%d" % k, [P, n * PACK], F32) for k, (c0, n) in enumerate(chunks)]
+        xb1.append(tile("xb1_last", [P, QUARTER * PACK], BF16, "th0"))
         hb = tile("hb", [P, HALF * PACK], BF16)
         h_codes = tile("hc", [P, S], U32)
         h_plane = tile("hs", [P, S], U8)
@@ -142,6 +143,8 @@ def tile_list_camera_error_maps_kernel(tc, xT, wgt, offs, w1, gain, w2_words, w2
                 return xb0[:, c0 * PACK : (c0 + n) * PACK]
             if c0 < QUARTER:
                 return xb1[0][:]
+            if c0 == 3 * QUARTER:
+                return xb1[2][:]
             return xb1[1][:, (c0 - QUARTER) * PACK : (c0 - QUARTER + n) * PACK]
 
         def weave_pair(a, i0, c0, n):
@@ -192,8 +195,10 @@ def tile_list_camera_error_maps_kernel(tc, xT, wgt, offs, w1, gain, w2_words, w2
             encode_pass(2 * q + 1, 1)
 
         def tanh(b):
+            k = b if b < 2 else b // 2 + 1
+            first = b * BANK - chunks[k][0] * PACK
             nc.scalar.activation(
-                th[:, b * BANK : (b + 1) * BANK].rearrange("p (n t) -> p n t", t=PACK),
+                th[k][:, first : first + BANK].rearrange("p (n t) -> p n t", t=PACK),
                 banks[b][:].rearrange("p t n -> p n t"),
                 ACT.Tanh,
             )
@@ -206,7 +211,7 @@ def tile_list_camera_error_maps_kernel(tc, xT, wgt, offs, w1, gain, w2_words, w2
             c0, n = chunks[k]
             engine.tensor_tensor(
                 rounded_h(k).rearrange("p (n t) -> p n t", t=PACK),
-                th[:, c0 * PACK : (c0 + n) * PACK].rearrange("p (n t) -> p n t", t=PACK),
+                th[k][:].rearrange("p (n t) -> p n t", t=PACK),
                 gain_sb[:].unsqueeze(1).to_broadcast([P, n, PACK]),
                 ALU.mult,
             )
@@ -276,32 +281,37 @@ def tile_list_camera_error_maps_kernel(tc, xT, wgt, offs, w1, gain, w2_words, w2
         quant_w1(1)
         encode_pass(0, 1)
         encode_pass(1, 1)
-        for q in range(1, 4):
-            weave_four(1, q * QUARTER, QUARTER)
+        weave_four(1, QUARTER, QUARTER)
+        weave_four(1, 2 * QUARTER, QUARTER)
         deal_w2_words()
         close_quarter(1)
         deal_w2_scales()
         close_quarter(2)
-        for b in range(6):
-            tanh(b)
+        tanh(0)
+        tanh(1)
         apply_gain(0, nc.vector)
-        close_quarter(3)
-        quant_h(0)
+        tanh(2)
+        tanh(3)
+        weave_four(1, 3 * QUARTER, QUARTER)
+        tanh(4)
+        tanh(5)
         apply_gain(1, nc.vector)
-        apply_gain(2, nc.vector)
+        quant_h(0)
         quant_h(1)
+        apply_gain(2, nc.vector)
         subtract(0, 0, 0, PACK)
+        finish(*chunks[0], 0, 0, PACK)
+        close_quarter(3)
         quant_h(2)
         apply_gain(3, nc.gpsimd)
-        finish(*chunks[0], 0, 0, PACK)
         subtract(1, 0, 0, PACK)
         finish(*chunks[1], 0, 0, PACK)
         subtract(0, 1, 0, PACK)
         subtract(1, 1, 0, PACK)
         finish(0, QUARTER, 1, 0, PACK)
+        errors_pass(2, 0)
         tanh(6)
         tanh(7)
-        errors_pass(2, 0)
         quant_h(3)
         apply_gain(4, nc.gpsimd)
         errors_pass(2, 1)

@@ -26,6 +26,7 @@ QUARTER = S // 4
 N1 = BANK // PACK
 CAMERAS = 8
 GROUP = 16
+RING = 3
 
 
 def tile_list_camera_error_maps_kernel(tc, xT, wgt, offs, w1, gain, w2_words, w2_scales, prec, out):
@@ -38,7 +39,7 @@ def tile_list_camera_error_maps_kernel(tc, xT, wgt, offs, w1, gain, w2_words, w2
     with ExitStack() as ctx:
         keep = ctx.enter_context(tc.tile_pool(name="keep", bufs=1))
         laid = ctx.enter_context(tc.tile_pool(name="laid", bufs=1))
-        psum = ctx.enter_context(tc.psum_pool(name="psum", bufs=8))
+        psum = ctx.enter_context(tc.psum_pool(name="psum", bufs=1))
 
         def tile(name, shape, dtype, tag=None):
             return keep.tile(shape, dtype, name=name, tag=tag or name, align_bytes=64)
@@ -57,11 +58,11 @@ def tile_list_camera_error_maps_kernel(tc, xT, wgt, offs, w1, gain, w2_words, w2
         xg = [tile("xg%d" % a, [P, PACK, S], F32) for a in range(PASSES)]
         xb0 = tile("xb0", [P, S * PACK], BF16)
         xb1 = [tile("xb1_front", [P, QUARTER * PACK], BF16, "w1raw0"), tile("xb1_back", [P, HALF * PACK], BF16, "w1raw2")]
-        x0_codes = tile("xc0", [P, S], U32, "x11")
+        x0_codes = tile("xc0", [P, S], U32, "x10")
         x_plane = [tile("xs%d" % a, [P, S], U8) for a in range(PASSES)]
         w1b = [tile("w1b0", [P, H * PACK], BF16), laid.tile([P, H * PACK], BF16, name="w1b1", offset=0, align_bytes=64)]
         x1_codes = [
-            tile("xc10", [P, QUARTER], U32, "w1raw3"),
+            tile("xc10", [P, QUARTER], U32),
             laid.tile([P, QUARTER], U32, name="xc11", offset=3 * K, align_bytes=64),
             tile("xc12", [P, QUARTER], U32),
             tile("xc13", [P, QUARTER], U32),
@@ -105,22 +106,22 @@ def tile_list_camera_error_maps_kernel(tc, xT, wgt, offs, w1, gain, w2_words, w2
         nc.scalar.dma_start(gain_sb[:], gain.rearrange("(p t) -> p t", t=PACK))
         nc.scalar.dma_start(prec_sb[:], prec.rearrange("(a p i) -> p a i", a=PASSES, i=PACK))
 
-        spreads = [(0, 2, nc.vector.tensor_copy), (2, 2, nc.scalar.copy), (4, 4, nc.scalar.copy)]
+        spreads = [(0, 2, nc.vector.tensor_copy), (2, 2, nc.scalar.copy), (4, 2, nc.scalar.copy), (6, 2, nc.scalar.copy)]
         for h in range(2):
-            turned = psum.tile([P, P], F32, name="turned", tag="bank")
+            turned = psum.tile([P, P], F32, name="turned", tag="bank%d" % h)
             nc.tensor.transpose(turned[:], wgt_rows[:], identity[:])
-            for c0, n, copy in spreads[h : 2 * h + 1]:
+            for c0, n, copy in spreads[h : 3 * h + 1]:
                 copy(
                     wgt_spread[:, c0 * P : (c0 + n) * P].rearrange("p (c g r) -> p c g r", g=CAMERAS, r=GROUP),
                     turned[:, 0 : P // 2].rearrange("p (g c) -> p c g", g=CAMERAS)[:, c0 : c0 + n, :].unsqueeze(3).to_broadcast([P, n, CAMERAS, GROUP]),
                 )
         for c0, n, copy in spreads:
-            back = psum.tile([P, n * P], F32, name="back", tag="bank")
+            back = psum.tile([P, n * P], F32, name="back", tag="bank%d" % (2 + c0 // 2))
             for c in range(n):
                 nc.tensor.transpose(back[:, c * P : (c + 1) * P], wgt_spread[:, (c0 + c) * P : (c0 + c + 1) * P], identity[:])
             copy(wgt_sb[:, c0 * P : (c0 + n) * P], back[:])
 
-        banks = [psum.tile([P, PACK, N1], F32, name="hbank%d" % b, tag="bank") for b in range(S // N1)]
+        banks = [psum.tile([P, PACK, N1], F32, name="hbank%d" % b, tag="bank%d" % b) for b in range(S // N1)]
 
         def deal_w2_words():
             nc.vector.tensor_copy(
@@ -220,10 +221,13 @@ def tile_list_camera_error_maps_kernel(tc, xT, wgt, offs, w1, gain, w2_words, w2
             c0, n = chunks[k]
             nc.vector.quantize_mx(h_codes[:, c0 : c0 + n].bitcast(E4M3X4), h_plane[:, c0 : c0 + n], rounded_h(k))
 
+        decoded = []
+
         def subtract(k, a, i0, count):
             c0, n = chunks[k]
             cols = slice(c0, c0 + n)
-            bank = psum.tile([P, count, n], F32, name="rbank", tag="bank")
+            bank = psum.tile([P, count, n], F32, name="rbank", tag="bank%d" % (len(decoded) % RING))
+            decoded.append(bank)
             for u in range(count):
                 g = a * PACK + i0 + u
                 nc.tensor.matmul_mx(
@@ -249,14 +253,12 @@ def tile_list_camera_error_maps_kernel(tc, xT, wgt, offs, w1, gain, w2_words, w2
             square(c0, n, a, i0, count)
             store(c0, n, a, i0, count, queue)
 
-        def errors_pass(k, a):
-            for i0 in (0, 2):
-                subtract(k, a, i0, 2)
-                square(*chunks[k], a, i0, 2)
-            store(*chunks[k], a, 0, PACK)
+        def errors(k, a, i0):
+            subtract(k, a, i0, 2)
+            finish(*chunks[k], a, i0, 2)
 
-        for c0, n, copy in spreads:
-            gather(0, 0, c0 * P, n * P)
+        for c0, n in ((0, QUARTER), (QUARTER, QUARTER), (HALF, QUARTER), (3 * QUARTER, QUARTER)):
+            gather(0, 0, c0, n)
         gather(0, 1, 0, S)
         weave_pair(0, 0, 0, S)
         gather(0, 2, 0, S)
@@ -272,8 +274,8 @@ def tile_list_camera_error_maps_kernel(tc, xT, wgt, offs, w1, gain, w2_words, w2
         quant_w1(0)
         for b in range(S // N1):
             encode_pass(b, 0)
-        for q in range(4):
-            gather(1, 3, q * QUARTER, QUARTER)
+        for c0, n in ((0, QUARTER), (QUARTER, QUARTER), (HALF, HALF)):
+            gather(1, 3, c0, n)
         weave_pair(1, 2, 0, QUARTER)
         cast_w1(2, nc.scalar.copy)
         cast_w1(3, nc.vector.tensor_copy)
@@ -299,28 +301,29 @@ def tile_list_camera_error_maps_kernel(tc, xT, wgt, offs, w1, gain, w2_words, w2
         quant_h(0)
         quant_h(1)
         apply_gain(2, nc.vector)
-        subtract(0, 0, 0, PACK)
-        finish(*chunks[0], 0, 0, PACK)
         close_quarter(3)
         quant_h(2)
         apply_gain(3, nc.gpsimd)
+        tanh(6)
+        subtract(0, 0, 0, PACK)
+        finish(*chunks[0], 0, 0, PACK)
         subtract(1, 0, 0, PACK)
         finish(*chunks[1], 0, 0, PACK)
-        subtract(0, 1, 0, PACK)
-        subtract(1, 1, 0, PACK)
-        finish(0, QUARTER, 1, 0, PACK)
-        errors_pass(2, 0)
-        tanh(6)
         tanh(7)
+        for k in range(2):
+            subtract(k, 1, 0, PACK)
+            finish(*chunks[k], 1, 0, PACK)
+        errors(2, 0, 0)
         quant_h(3)
         apply_gain(4, nc.gpsimd)
-        errors_pass(2, 1)
-        errors_pass(3, 0)
-        subtract(3, 1, 0, 2)
-        finish(*chunks[3], 1, 0, 2)
+        errors(2, 0, 2)
+        for k, a in ((2, 1), (3, 0)):
+            errors(k, a, 0)
+            errors(k, a, 2)
         quant_h(4)
-        subtract(3, 1, 2, 2)
-        finish(*chunks[3], 1, 2, 2)
+        for i0 in (0, 2):
+            subtract(3, 1, i0, 2)
+            finish(*chunks[3], 1, i0, 2)
         for i0 in (0, 2):
             subtract(4, 0, i0, 2)
             finish(*chunks[4], 0, i0, 2)

@@ -38,7 +38,6 @@ def tile_list_camera_error_maps_kernel(tc, xT, wgt, offs, w1, gain, w2_words, w2
 
     with ExitStack() as ctx:
         keep = ctx.enter_context(tc.tile_pool(name="keep", bufs=1))
-        laid = ctx.enter_context(tc.tile_pool(name="laid", bufs=1))
         psum = ctx.enter_context(tc.psum_pool(name="psum", bufs=1))
 
         def tile(name, shape, dtype, tag=None):
@@ -60,19 +59,19 @@ def tile_list_camera_error_maps_kernel(tc, xT, wgt, offs, w1, gain, w2_words, w2
         xb1 = [tile("xb1_front", [P, QUARTER * PACK], BF16, "w1raw0"), tile("xb1_back", [P, HALF * PACK], BF16, "w1raw2")]
         x0_codes = tile("xc0", [P, S], U32, "x10")
         x_plane = [tile("xs%d" % a, [P, S], U8) for a in range(PASSES)]
-        w1b = [tile("w1b0", [P, H * PACK], BF16), laid.tile([P, H * PACK], BF16, name="w1b1", offset=0, align_bytes=64)]
+        w1b = [tile("w1b0", [P, H * PACK], BF16), tile("w1b1", [P, H * PACK], BF16)]
         x1_codes = [
             tile("xc10", [P, QUARTER], U32),
-            laid.tile([P, QUARTER], U32, name="xc11", offset=3 * K, align_bytes=64),
+            tile("xc11", [P, QUARTER], U32),
             tile("xc12", [P, QUARTER], U32),
             tile("xc13", [P, QUARTER], U32),
         ]
         w1_codes = [tile("w1c%d" % a, [P, H], U32) for a in range(PASSES)]
         w1_plane = [tile("w1s%d" % a, [P, H], U8) for a in range(PASSES)]
-        w2_codes = laid.tile([P, 2 * K], U8, name="w2_codes", offset=0, align_bytes=64)
-        w2_plane = laid.tile([P, K], U8, name="w2_plane", offset=2 * K, align_bytes=64)
+        w2_codes = tile("w2_codes", [P, 2 * K], U8)
+        w2_plane = tile("w2_plane", [P, K], U8)
         th = [tile("th%d" % k, [P, n * PACK], F32) for k, (c0, n) in enumerate(chunks)]
-        xb1.append(tile("xb1_last", [P, QUARTER * PACK], BF16, "th0"))
+        xb1.append(tile("xb1_last", [P, QUARTER * PACK], BF16, "w1b1"))
         hb = tile("hb", [P, HALF * PACK], BF16)
         h_codes = tile("hc", [P, S], U32)
         h_plane = tile("hs", [P, S], U8)
@@ -154,8 +153,8 @@ def tile_list_camera_error_maps_kernel(tc, xT, wgt, offs, w1, gain, w2_words, w2
                 xg[a][:, i0 : i0 + 2, c0 : c0 + n].rearrange("p i c -> p c i"),
             )
 
-        def weave_four(a, c0, n):
-            nc.scalar.copy(
+        def weave_four(a, c0, n, copy=nc.scalar.copy):
+            copy(
                 rounded_x(a, c0, n).rearrange("p (c e i) -> p c i e", e=PACK, i=PACK),
                 xg[a][:, :, c0 : c0 + n].rearrange("p i (c e) -> p c i e", e=PACK),
             )
@@ -253,10 +252,6 @@ def tile_list_camera_error_maps_kernel(tc, xT, wgt, offs, w1, gain, w2_words, w2
             square(c0, n, a, i0, count)
             store(c0, n, a, i0, count, queue)
 
-        def errors(k, a, i0):
-            subtract(k, a, i0, 2)
-            finish(*chunks[k], a, i0, 2)
-
         for c0, n in ((0, QUARTER), (QUARTER, QUARTER), (HALF, QUARTER), (3 * QUARTER, QUARTER)):
             gather(0, 0, c0, n)
         gather(0, 1, 0, S)
@@ -278,55 +273,59 @@ def tile_list_camera_error_maps_kernel(tc, xT, wgt, offs, w1, gain, w2_words, w2
             gather(1, 3, c0, n)
         weave_pair(1, 2, 0, QUARTER)
         cast_w1(2, nc.scalar.copy)
-        cast_w1(3, nc.vector.tensor_copy)
         quant_x(1, 0, QUARTER)
+        cast_w1(3, nc.vector.tensor_copy)
+        deal_w2_words()
         quant_w1(1)
         encode_pass(0, 1)
         encode_pass(1, 1)
         weave_four(1, QUARTER, QUARTER)
         weave_four(1, 2 * QUARTER, QUARTER)
-        deal_w2_words()
         close_quarter(1)
-        deal_w2_scales()
+        weave_four(1, 3 * QUARTER, QUARTER, nc.vector.tensor_copy)
         close_quarter(2)
-        tanh(0)
-        tanh(1)
+        close_quarter(3)
+        deal_w2_scales()
+        for b in range(8):
+            tanh(b)
         apply_gain(0, nc.vector)
-        tanh(2)
-        tanh(3)
-        weave_four(1, 3 * QUARTER, QUARTER)
-        tanh(4)
-        tanh(5)
         apply_gain(1, nc.vector)
         quant_h(0)
         quant_h(1)
         apply_gain(2, nc.vector)
-        close_quarter(3)
+        subtract(0, 0, 0, 4)
+        finish(*chunks[0], 0, 0, 4)
         quant_h(2)
         apply_gain(3, nc.gpsimd)
-        tanh(6)
-        subtract(0, 0, 0, PACK)
-        finish(*chunks[0], 0, 0, PACK)
-        subtract(1, 0, 0, PACK)
-        finish(*chunks[1], 0, 0, PACK)
-        tanh(7)
-        for k in range(2):
-            subtract(k, 1, 0, PACK)
-            finish(*chunks[k], 1, 0, PACK)
-        errors(2, 0, 0)
+        subtract(1, 0, 0, 4)
+        finish(*chunks[1], 0, 0, 4)
+        subtract(0, 1, 0, 4)
+        finish(*chunks[0], 1, 0, 4)
+        subtract(1, 1, 0, 4)
+        finish(*chunks[1], 1, 0, 4)
+        subtract(2, 0, 0, 2)
+        finish(*chunks[2], 0, 0, 2)
+        subtract(2, 0, 2, 2)
+        finish(*chunks[2], 0, 2, 2)
         quant_h(3)
         apply_gain(4, nc.gpsimd)
-        errors(2, 0, 2)
-        for k, a in ((2, 1), (3, 0)):
-            errors(k, a, 0)
-            errors(k, a, 2)
+        subtract(2, 1, 0, 2)
+        finish(*chunks[2], 1, 0, 2)
+        subtract(2, 1, 2, 2)
+        finish(*chunks[2], 1, 2, 2)
+        subtract(3, 0, 0, 2)
+        finish(*chunks[3], 0, 0, 2)
+        subtract(3, 0, 2, 2)
+        finish(*chunks[3], 0, 2, 2)
+        subtract(3, 1, 0, 2)
+        finish(*chunks[3], 1, 0, 2)
         quant_h(4)
-        for i0 in (0, 2):
-            subtract(3, 1, i0, 2)
-            finish(*chunks[3], 1, i0, 2)
-        for i0 in (0, 2):
-            subtract(4, 0, i0, 2)
-            finish(*chunks[4], 0, i0, 2)
+        subtract(3, 1, 2, 2)
+        finish(*chunks[3], 1, 2, 2)
+        subtract(4, 0, 0, 2)
+        finish(*chunks[4], 0, 0, 2)
+        subtract(4, 0, 2, 2)
+        finish(*chunks[4], 0, 2, 2)
         subtract(4, 1, 0, 2)
         finish(*chunks[4], 1, 0, 2)
         subtract(4, 1, 2, 1)

@@ -207,11 +207,11 @@ def tile_list_camera_error_maps_kernel(tc, xT, wgt, offs, w1, gain, w2_words, w2
             first = min(chunks[k][0], QUARTER) * PACK
             return hb[:, first : first + chunks[k][1] * PACK]
 
-        def apply_gain(k, engine):
-            c0, n = chunks[k]
+        def apply_gain(k, engine, first=0, n=None):
+            n = n or chunks[k][1]
             engine.tensor_tensor(
-                rounded_h(k).rearrange("p (n t) -> p n t", t=PACK),
-                th[k][:].rearrange("p (n t) -> p n t", t=PACK),
+                rounded_h(k).rearrange("p (n t) -> p n t", t=PACK)[:, first : first + n, :],
+                th[k][:].rearrange("p (n t) -> p n t", t=PACK)[:, first : first + n, :],
                 gain_sb[:].unsqueeze(1).to_broadcast([P, n, PACK]),
                 ALU.mult,
             )
@@ -291,8 +291,9 @@ def tile_list_camera_error_maps_kernel(tc, xT, wgt, offs, w1, gain, w2_words, w2
         apply_gain(0, nc.vector)
         apply_gain(1, nc.vector)
         quant_h(0)
+        apply_gain(2, nc.vector, 0, N1)
         quant_h(1)
-        apply_gain(2, nc.vector)
+        apply_gain(2, nc.vector, N1, N1)
         subtract(0, 0, 0, 4)
         finish(*chunks[0], 0, 0, 4)
         quant_h(2)

@@ -38,6 +38,7 @@ def tile_list_camera_error_maps_kernel(tc, xT, wgt, offs, w1, gain, w2_words, w2
 
     with ExitStack() as ctx:
         keep = ctx.enter_context(tc.tile_pool(name="keep", bufs=1))
+        laid = ctx.enter_context(tc.tile_pool(name="laid", bufs=1))
         psum = ctx.enter_context(tc.psum_pool(name="psum", bufs=1))
 
         def tile(name, shape, dtype, tag=None):
@@ -59,7 +60,7 @@ def tile_list_camera_error_maps_kernel(tc, xT, wgt, offs, w1, gain, w2_words, w2
         xb1 = [tile("xb1_front", [P, QUARTER * PACK], BF16, "w1raw0"), tile("xb1_back", [P, HALF * PACK], BF16, "w1raw2")]
         x0_codes = tile("xc0", [P, S], U32, "x10")
         x_plane = [tile("xs%d" % a, [P, S], U8) for a in range(PASSES)]
-        w1b = [tile("w1b0", [P, H * PACK], BF16), tile("w1b1", [P, H * PACK], BF16)]
+        w1b = [tile("w1b0", [P, H * PACK], BF16), laid.tile([P, H * PACK], BF16, name="w1b1", offset=0, align_bytes=64)]
         x1_codes = [
             tile("xc10", [P, QUARTER], U32),
             tile("xc11", [P, QUARTER], U32),
@@ -69,9 +70,9 @@ def tile_list_camera_error_maps_kernel(tc, xT, wgt, offs, w1, gain, w2_words, w2
         w1_codes = [tile("w1c%d" % a, [P, H], U32) for a in range(PASSES)]
         w1_plane = [tile("w1s%d" % a, [P, H], U8) for a in range(PASSES)]
         w2_codes = tile("w2_codes", [P, 2 * K], U8)
-        w2_plane = tile("w2_plane", [P, K], U8)
+        w2_plane = laid.tile([P, K], U8, name="w2_plane", offset=2 * K, align_bytes=64)
         th = [tile("th%d" % k, [P, n * PACK], F32) for k, (c0, n) in enumerate(chunks)]
-        xb1.append(tile("xb1_last", [P, QUARTER * PACK], BF16, "w1b1"))
+        xb1.append(laid.tile([P, QUARTER * PACK], BF16, name="xb1_last", offset=0, align_bytes=64))
         hb = tile("hb", [P, HALF * PACK], BF16)
         h_codes = tile("hc", [P, S], U32)
         h_plane = tile("hs", [P, S], U8)
@@ -83,8 +84,8 @@ def tile_list_camera_error_maps_kernel(tc, xT, wgt, offs, w1, gain, w2_words, w2
             r0 = k % 2 * (H // 2)
             nc.sync.dma_start(w1_raw[k][:], w1_rows[k // 2][:, :, r0 : r0 + H // 2])
 
-        nc.vector.memset(wgt_rows[P // 2 : P, :], 0.0)
         nc.vector.memset(s2_raw[:].bitcast(U32), 0)
+        nc.vector.memset(wgt_rows[P // 2 : P, :], 0.0)
         make_identity(nc, identity[:])
         nc.sync.dma_start(wgt_rows[0 : P // 2, :], wgt.rearrange("(g r) (c e) -> r g c e", r=GROUP, e=P)[0])
         nc.sync.dma_start(offsets[:], offs)
@@ -99,11 +100,11 @@ def tile_list_camera_error_maps_kernel(tc, xT, wgt, offs, w1, gain, w2_words, w2
         load_w1(2)
         load_w1(3)
         nc.sync.dma_start(w2_raw[:].bitcast(I32), w2_words[0].bitcast(I32))
+        nc.sync.dma_start(gain_sb[:], gain.rearrange("(p t) -> p t", t=PACK))
+        nc.sync.dma_start(prec_sb[:], prec.rearrange("(a p i) -> p a i", a=PASSES, i=PACK))
         scale_rows = w2_scales[0].bitcast(I32).rearrange("(q r) c -> r q c", r=4)
         for r in range(4):
-            nc.sync.dma_start(s2_raw[r:P:32, :].bitcast(I32), scale_rows[r])
-        nc.scalar.dma_start(gain_sb[:], gain.rearrange("(p t) -> p t", t=PACK))
-        nc.scalar.dma_start(prec_sb[:], prec.rearrange("(a p i) -> p a i", a=PASSES, i=PACK))
+            nc.scalar.dma_start(s2_raw[r:P:32, :].bitcast(I32), scale_rows[r])
 
         spreads = [(0, 2, nc.vector.tensor_copy), (2, 2, nc.scalar.copy), (4, 2, nc.scalar.copy), (6, 2, nc.scalar.copy)]
         for h in range(2):
@@ -283,9 +284,11 @@ def tile_list_camera_error_maps_kernel(tc, xT, wgt, offs, w1, gain, w2_words, w2
         weave_four(1, 2 * QUARTER, QUARTER)
         close_quarter(1)
         weave_four(1, 3 * QUARTER, QUARTER, nc.vector.tensor_copy)
-        close_quarter(2)
-        close_quarter(3)
         deal_w2_scales()
+        quant_x(1, 3 * QUARTER, QUARTER)
+        close_quarter(2)
+        encode_pass(6, 1)
+        encode_pass(7, 1)
         for b in range(8):
             tanh(b)
         apply_gain(0, nc.vector)

@@ -57,7 +57,7 @@ def tile_list_camera_error_maps_kernel(tc, xT, wgt, offs, w1, gain, w2_words, w2
         prec_sb = tile("prec_sb", [P, PASSES, PACK], F32)
         xg = [tile("xg%d" % a, [P, PACK, S], F32) for a in range(PASSES)]
         xb0 = tile("xb0", [P, S * PACK], BF16)
-        xb1 = [tile("xb1_front", [P, QUARTER * PACK], BF16, "w1raw0"), tile("xb1_back", [P, HALF * PACK], BF16, "w1raw2")]
+        xb1 = [tile("xb1_front", [P, QUARTER * PACK], BF16, "w1raw0"), tile("xb1_back", [P, HALF * PACK], BF16)]
         x0_codes = tile("xc0", [P, S], U32, "x10")
         x_plane = [tile("xs%d" % a, [P, S], U8) for a in range(PASSES)]
         w1b = [tile("w1b0", [P, H * PACK], BF16), laid.tile([P, H * PACK], BF16, name="w1b1", offset=0, align_bytes=64)]
@@ -143,9 +143,9 @@ def tile_list_camera_error_maps_kernel(tc, xT, wgt, offs, w1, gain, w2_words, w2
             if a == 0:
                 return xb0[:, c0 * PACK : (c0 + n) * PACK]
             if c0 < QUARTER:
-                return xb1[0][:]
-            if c0 == 3 * QUARTER:
-                return xb1[2][:]
+                return xb1[0][:, c0 * PACK : (c0 + n) * PACK]
+            if c0 >= 3 * QUARTER:
+                return xb1[2][:, (c0 - 3 * QUARTER) * PACK : (c0 - 3 * QUARTER + n) * PACK]
             return xb1[1][:, (c0 - QUARTER) * PACK : (c0 - QUARTER + n) * PACK]
 
         def weave_pair(a, i0, c0, n):
@@ -270,9 +270,10 @@ def tile_list_camera_error_maps_kernel(tc, xT, wgt, offs, w1, gain, w2_words, w2
         quant_w1(0)
         for b in range(S // N1):
             encode_pass(b, 0)
-        for c0, n in ((0, QUARTER), (QUARTER, QUARTER), (HALF, HALF)):
+        for c0, n in ((0, N1), (N1, N1), (QUARTER, 3 * QUARTER)):
             gather(1, 3, c0, n)
-        weave_pair(1, 2, 0, QUARTER)
+        weave_pair(1, 2, 0, N1)
+        weave_pair(1, 2, N1, N1)
         cast_w1(2, nc.scalar.copy)
         quant_x(1, 0, QUARTER)
         cast_w1(3, nc.vector.tensor_copy)
@@ -283,12 +284,11 @@ def tile_list_camera_error_maps_kernel(tc, xT, wgt, offs, w1, gain, w2_words, w2
         weave_four(1, QUARTER, QUARTER)
         weave_four(1, 2 * QUARTER, QUARTER)
         close_quarter(1)
-        weave_four(1, 3 * QUARTER, QUARTER, nc.vector.tensor_copy)
+        weave_four(1, 6 * N1, N1)
+        weave_four(1, 7 * N1, N1, nc.vector.tensor_copy)
         deal_w2_scales()
-        quant_x(1, 3 * QUARTER, QUARTER)
         close_quarter(2)
-        encode_pass(6, 1)
-        encode_pass(7, 1)
+        close_quarter(3)
         for b in range(8):
             tanh(b)
         apply_gain(0, nc.vector)

@@ -69,7 +69,7 @@ def tile_list_camera_error_maps_kernel(tc, xT, wgt, offs, w1, gain, w2_words, w2
         ]
         w1_codes = [tile("w1c%d" % a, [P, H], U32) for a in range(PASSES)]
         w1_plane = [tile("w1s%d" % a, [P, H], U8) for a in range(PASSES)]
-        w2_codes = tile("w2_codes", [P, 2 * K], U8)
+        w2_codes = tile("w2_codes", [P, 2 * K], U8, "x01")
         w2_plane = laid.tile([P, K], U8, name="w2_plane", offset=2 * K, align_bytes=64)
         th = [tile("th%d" % k, [P, n * PACK], F32) for k, (c0, n) in enumerate(chunks)]
         xb1.append(laid.tile([P, QUARTER * PACK], BF16, name="xb1_last", offset=0, align_bytes=64))
@@ -88,9 +88,11 @@ def tile_list_camera_error_maps_kernel(tc, xT, wgt, offs, w1, gain, w2_words, w2
         nc.vector.memset(wgt_rows[P // 2 : P, :], 0.0)
         make_identity(nc, identity[:])
         nc.sync.dma_start(wgt_rows[0 : P // 2, :], wgt.rearrange("(g r) (c e) -> r g c e", r=GROUP, e=P)[0])
+        load_x(0, 0)
         nc.sync.dma_start(offsets[:], offs)
-        for i in range(PACK):
+        for i in range(1, PACK):
             load_x(0, i)
+        nc.sync.dma_start(w2_raw[:].bitcast(I32), w2_words[0].bitcast(I32))
         load_x(1, 0)
         load_x(1, 1)
         load_w1(0)
@@ -99,24 +101,23 @@ def tile_list_camera_error_maps_kernel(tc, xT, wgt, offs, w1, gain, w2_words, w2
         load_x(1, 3)
         load_w1(2)
         load_w1(3)
-        nc.sync.dma_start(w2_raw[:].bitcast(I32), w2_words[0].bitcast(I32))
         nc.sync.dma_start(gain_sb[:], gain.rearrange("(p t) -> p t", t=PACK))
         nc.sync.dma_start(prec_sb[:], prec.rearrange("(a p i) -> p a i", a=PASSES, i=PACK))
         scale_rows = w2_scales[0].bitcast(I32).rearrange("(q r) c -> r q c", r=4)
         for r in range(4):
             nc.scalar.dma_start(s2_raw[r:P:32, :].bitcast(I32), scale_rows[r])
 
-        spreads = [(0, 2, nc.vector.tensor_copy), (2, 2, nc.scalar.copy), (4, 2, nc.scalar.copy), (6, 2, nc.scalar.copy)]
+        spreads = [(0, 1, nc.vector.tensor_copy), (1, 1, nc.vector.tensor_copy), (2, 2, nc.scalar.copy), (4, 2, nc.scalar.copy), (6, 2, nc.scalar.copy)]
         for h in range(2):
             turned = psum.tile([P, P], F32, name="turned", tag="bank%d" % h)
             nc.tensor.transpose(turned[:], wgt_rows[:], identity[:])
-            for c0, n, copy in spreads[h : 3 * h + 1]:
+            for c0, n, copy in spreads[2 * h : 3 * h + 2]:
                 copy(
                     wgt_spread[:, c0 * P : (c0 + n) * P].rearrange("p (c g r) -> p c g r", g=CAMERAS, r=GROUP),
                     turned[:, 0 : P // 2].rearrange("p (g c) -> p c g", g=CAMERAS)[:, c0 : c0 + n, :].unsqueeze(3).to_broadcast([P, n, CAMERAS, GROUP]),
                 )
-        for c0, n, copy in spreads:
-            back = psum.tile([P, n * P], F32, name="back", tag="bank%d" % (2 + c0 // 2))
+        for part, (c0, n, copy) in enumerate(spreads):
+            back = psum.tile([P, n * P], F32, name="back", tag="bank%d" % (2 + part))
             for c in range(n):
                 nc.tensor.transpose(back[:, c * P : (c + 1) * P], wgt_spread[:, (c0 + c) * P : (c0 + c + 1) * P], identity[:])
             copy(wgt_sb[:, c0 * P : (c0 + n) * P], back[:])
@@ -124,7 +125,7 @@ def tile_list_camera_error_maps_kernel(tc, xT, wgt, offs, w1, gain, w2_words, w2
         banks = [psum.tile([P, PACK, N1], F32, name="hbank%d" % b, tag="bank%d" % b) for b in range(S // N1)]
 
         def deal_w2_words():
-            nc.vector.tensor_copy(
+            nc.scalar.copy(
                 w2_codes[:].bitcast(U16).rearrange("p (a i q) -> p a i q", a=PASSES, i=PACK),
                 w2_raw[:].bitcast(U16).rearrange("p (a q i) -> p a i q", a=PASSES, i=PACK),
             )
@@ -253,10 +254,11 @@ def tile_list_camera_error_maps_kernel(tc, xT, wgt, offs, w1, gain, w2_words, w2
             square(c0, n, a, i0, count)
             store(c0, n, a, i0, count, queue)
 
-        for c0, n in ((0, QUARTER), (QUARTER, QUARTER), (HALF, QUARTER), (3 * QUARTER, QUARTER)):
+        for c0, n in ((0, N1), (N1, N1), (QUARTER, QUARTER), (HALF, QUARTER), (3 * QUARTER, QUARTER)):
             gather(0, 0, c0, n)
         gather(0, 1, 0, S)
         weave_pair(0, 0, 0, S)
+        deal_w2_words()
         gather(0, 2, 0, S)
         gather(0, 3, 0, S)
         weave_pair(0, 2, 0, S)
@@ -277,15 +279,13 @@ def tile_list_camera_error_maps_kernel(tc, xT, wgt, offs, w1, gain, w2_words, w2
         cast_w1(2, nc.scalar.copy)
         quant_x(1, 0, QUARTER)
         cast_w1(3, nc.vector.tensor_copy)
-        deal_w2_words()
         quant_w1(1)
         encode_pass(0, 1)
         encode_pass(1, 1)
         weave_four(1, QUARTER, QUARTER)
         weave_four(1, 2 * QUARTER, QUARTER)
         close_quarter(1)
-        weave_four(1, 6 * N1, N1)
-        weave_four(1, 7 * N1, N1, nc.vector.tensor_copy)
+        weave_four(1, 3 * QUARTER, QUARTER, nc.vector.tensor_copy)
         deal_w2_scales()
         close_quarter(2)
         close_quarter(3)

@@ -50,7 +50,8 @@ def tile_list_camera_error_maps_kernel(tc, xT, wgt, offs, w1, gain, w2_words, w2
         wgt_sb = tile("wgt_sb", [P, S], F32)
         identity = tile("identity", [P, P], F32)
         x_sb = [[tile("x%d%d" % (a, i), [P, T], F32) for i in range(PACK)] for a in range(PASSES)]
-        w1_raw = [tile("w1raw%d" % k, [P, PACK, H // 2], F32) for k in range(2 * PASSES)]
+        w1_raw = [tile("w1raw%d" % k, [P, PACK, H // 2], F32) for k in range(2 * PASSES) if k != 2]
+        w1_raw = w1_raw[0:2] + [laid.tile([P, PACK, H // 2], F32, name="w1raw2", offset=0, align_bytes=64)] + w1_raw[2:]
         w2_raw = tile("w2_raw", [P, 2 * K], U8)
         s2_raw = tile("s2_raw", [P, K], U8)
         gain_sb = tile("gain_sb", [P, PACK], F32)
@@ -60,7 +61,7 @@ def tile_list_camera_error_maps_kernel(tc, xT, wgt, offs, w1, gain, w2_words, w2
         xb1 = [tile("xb1_front", [P, QUARTER * PACK], BF16, "w1raw0"), tile("xb1_back", [P, HALF * PACK], BF16)]
         x0_codes = tile("xc0", [P, S], U32, "x10")
         x_plane = [tile("xs%d" % a, [P, S], U8) for a in range(PASSES)]
-        w1b = [tile("w1b0", [P, H * PACK], BF16), laid.tile([P, H * PACK], BF16, name="w1b1", offset=0, align_bytes=64)]
+        w1b = [tile("w1b0", [P, H * PACK], BF16), tile("w1b1", [P, H * PACK], BF16)]
         x1_codes = [
             tile("xc10", [P, QUARTER], U32),
             tile("xc11", [P, QUARTER], U32),
@@ -279,14 +280,14 @@ def tile_list_camera_error_maps_kernel(tc, xT, wgt, offs, w1, gain, w2_words, w2
         cast_w1(2, nc.scalar.copy)
         quant_x(1, 0, QUARTER)
         cast_w1(3, nc.vector.tensor_copy)
+        deal_w2_scales()
         quant_w1(1)
         encode_pass(0, 1)
         encode_pass(1, 1)
         weave_four(1, QUARTER, QUARTER)
         weave_four(1, 2 * QUARTER, QUARTER)
-        close_quarter(1)
         weave_four(1, 3 * QUARTER, QUARTER, nc.vector.tensor_copy)
-        deal_w2_scales()
+        close_quarter(1)
         close_quarter(2)
         close_quarter(3)
         for b in range(8):

@@ -58,7 +58,11 @@ def tile_list_camera_error_maps_kernel(tc, xT, wgt, offs, w1, gain, w2_words, w2
         prec_sb = tile("prec_sb", [P, PASSES, PACK], F32)
         xg = [tile("xg%d" % a, [P, PACK, S], F32) for a in range(PASSES)]
         xb0 = tile("xb0", [P, S * PACK], BF16)
-        xb1 = [tile("xb1_front", [P, QUARTER * PACK], BF16, "w1raw0"), tile("xb1_back", [P, HALF * PACK], BF16)]
+        xb1 = [
+            tile("xb1_front", [P, QUARTER * PACK], BF16, "w1raw0"),
+            tile("xb1_second", [P, QUARTER * PACK], BF16),
+            tile("xb1_third", [P, QUARTER * PACK], BF16, "w1raw1"),
+        ]
         x0_codes = tile("xc0", [P, S], U32, "x10")
         x_plane = [tile("xs%d" % a, [P, S], U8) for a in range(PASSES)]
         w1b = [tile("w1b0", [P, H * PACK], BF16), tile("w1b1", [P, H * PACK], BF16)]
@@ -144,11 +148,7 @@ def tile_list_camera_error_maps_kernel(tc, xT, wgt, offs, w1, gain, w2_words, w2
         def rounded_x(a, c0, n):
             if a == 0:
                 return xb0[:, c0 * PACK : (c0 + n) * PACK]
-            if c0 < QUARTER:
-                return xb1[0][:, c0 * PACK : (c0 + n) * PACK]
-            if c0 >= 3 * QUARTER:
-                return xb1[2][:, (c0 - 3 * QUARTER) * PACK : (c0 - 3 * QUARTER + n) * PACK]
-            return xb1[1][:, (c0 - QUARTER) * PACK : (c0 - QUARTER + n) * PACK]
+            return xb1[c0 // QUARTER][:, c0 % QUARTER * PACK : (c0 % QUARTER + n) * PACK]
 
         def weave_pair(a, i0, c0, n):
             nc.scalar.copy(
@@ -268,8 +268,10 @@ def tile_list_camera_error_maps_kernel(tc, xT, wgt, offs, w1, gain, w2_words, w2
         quant_x(0, 0, S)
         cast_w1(0, nc.scalar.copy)
         weave_pair(1, 0, 0, QUARTER)
+        weave_pair(1, 0, QUARTER, QUARTER)
         gather(1, 2, 0, S)
         cast_w1(1, nc.scalar.copy)
+        weave_pair(1, 0, HALF, QUARTER)
         quant_w1(0)
         for b in range(S // N1):
             encode_pass(b, 0)
@@ -280,13 +282,14 @@ def tile_list_camera_error_maps_kernel(tc, xT, wgt, offs, w1, gain, w2_words, w2
         cast_w1(2, nc.scalar.copy)
         quant_x(1, 0, QUARTER)
         cast_w1(3, nc.vector.tensor_copy)
-        deal_w2_scales()
+        weave_four(1, 7 * N1, N1, nc.vector.tensor_copy)
         quant_w1(1)
         encode_pass(0, 1)
         encode_pass(1, 1)
-        weave_four(1, QUARTER, QUARTER)
-        weave_four(1, 2 * QUARTER, QUARTER)
-        weave_four(1, 3 * QUARTER, QUARTER, nc.vector.tensor_copy)
+        weave_pair(1, 2, QUARTER, QUARTER)
+        weave_pair(1, 2, HALF, QUARTER)
+        weave_four(1, 6 * N1, N1)
+        deal_w2_scales()
         close_quarter(1)
         close_quarter(2)
         close_quarter(3)

@@ -177,8 +177,8 @@ def tile_list_camera_error_maps_kernel(tc, xT, wgt, offs, w1, gain, w2_words, w2
                 w1_raw[k][:].rearrange("p i (m t) -> p m i t", t=PACK),
             )
 
-        def quant_w1(a):
-            nc.vector.quantize_mx(w1_codes[a][:].bitcast(E4M3X4), w1_plane[a][:], w1b[a][:])
+        def quant_w1(a, c0=0, n=H):
+            nc.vector.quantize_mx(w1_codes[a][:, c0 : c0 + n].bitcast(E4M3X4), w1_plane[a][:, c0 : c0 + n], w1b[a][:, c0 * PACK : (c0 + n) * PACK])
 
         def encode_pass(b, a):
             for t in range(PACK):
@@ -197,12 +197,12 @@ def tile_list_camera_error_maps_kernel(tc, xT, wgt, offs, w1, gain, w2_words, w2
             encode_pass(2 * q, 1)
             encode_pass(2 * q + 1, 1)
 
-        def tanh(b):
+        def tanh(b, c0=0, n=N1):
             k = b if b < 2 else b // 2 + 1
             first = b * BANK - chunks[k][0] * PACK
             nc.scalar.activation(
-                th[k][:, first : first + BANK].rearrange("p (n t) -> p n t", t=PACK),
-                banks[b][:].rearrange("p t n -> p n t"),
+                th[k][:, first : first + BANK].rearrange("p (n t) -> p n t", t=PACK)[:, c0 : c0 + n, :],
+                banks[b][:].rearrange("p t n -> p n t")[:, c0 : c0 + n, :],
                 ACT.Tanh,
             )
 
@@ -283,7 +283,8 @@ def tile_list_camera_error_maps_kernel(tc, xT, wgt, offs, w1, gain, w2_words, w2
         quant_x(1, 0, QUARTER)
         cast_w1(3, nc.vector.tensor_copy)
         weave_four(1, 7 * N1, N1, nc.vector.tensor_copy)
-        quant_w1(1)
+        quant_w1(1, 0, H // 2)
+        quant_w1(1, H // 2, H // 2)
         encode_pass(0, 1)
         encode_pass(1, 1)
         weave_pair(1, 2, QUARTER, QUARTER)
@@ -293,9 +294,12 @@ def tile_list_camera_error_maps_kernel(tc, xT, wgt, offs, w1, gain, w2_words, w2
         close_quarter(1)
         close_quarter(2)
         close_quarter(3)
-        for b in range(8):
+        tanh(0, 0, N1 // 2)
+        tanh(0, N1 // 2, N1 // 2)
+        for b in range(1, 8):
             tanh(b)
-        apply_gain(0, nc.vector)
+        apply_gain(0, nc.vector, 0, N1 // 2)
+        apply_gain(0, nc.vector, N1 // 2, N1 // 2)
         apply_gain(1, nc.vector)
         quant_h(0)
         apply_gain(2, nc.vector, 0, N1)

from contextlib import ExitStack

import concourse.mybir as mybir
from concourse.masks import make_identity

K, T, S, H = 1024, 2048, 1024, 512
FLOPS = 2 * 2 * K * H * S

F32 = mybir.dt.float32
BF16 = mybir.dt.bfloat16
I32 = mybir.dt.int32
U32 = mybir.dt.uint32
U16 = mybir.dt.uint16
U8 = mybir.dt.uint8
E4M3X4 = mybir.dt.float8_e4m3fn_x4
E2M1X4 = mybir.dt.float4_e2m1fn_x4
ACT = mybir.ActivationFunctionType
ALU = mybir.AluOpType

P = 128
PACK = 4
PASSES = 2
BANK = 512
HALF = S // 2
QUARTER = S // 4
N1 = BANK // PACK
CAMERAS = 8
GROUP = 16
RING = 3


def tile_list_camera_error_maps_kernel(tc, xT, wgt, offs, w1, gain, w2_words, w2_scales, prec, out):
    nc = tc.nc
    x_planes = xT.rearrange("(a p i) t -> a i p t", a=PASSES, i=PACK)
    out_rows = out.rearrange("(a p i) j -> a p i j", a=PASSES, i=PACK)
    w1_rows = w1.rearrange("(a p i) r -> a p i r", a=PASSES, i=PACK)
    chunks = [(0, N1), (N1, N1), (QUARTER, QUARTER), (2 * QUARTER, QUARTER), (3 * QUARTER, QUARTER)]

    with ExitStack() as ctx:
        keep = ctx.enter_context(tc.tile_pool(name="keep", bufs=1))
        laid = ctx.enter_context(tc.tile_pool(name="laid", bufs=1))
        psum = ctx.enter_context(tc.psum_pool(name="psum", bufs=1))

        def tile(name, shape, dtype, tag=None):
            return keep.tile(shape, dtype, name=name, tag=tag or name, align_bytes=64)

        offsets = keep.tile([P, S // 16], U16, name="offsets")
        wgt_rows = tile("wgt_rows", [P, P], F32)
        wgt_spread = tile("wgt_spread", [P, S], F32)
        wgt_sb = tile("wgt_sb", [P, S], F32)
        identity = tile("identity", [P, P], F32)
        x_sb = [[tile("x%d%d" % (a, i), [P, T], F32) for i in range(PACK)] for a in range(PASSES)]
        w1_raw = [tile("w1raw%d" % k, [P, PACK, H // 2], F32) for k in range(2 * PASSES) if k != 2]
        w1_raw = w1_raw[0:2] + [laid.tile([P, PACK, H // 2], F32, name="w1raw2", offset=0, align_bytes=64)] + w1_raw[2:]
        w2_raw = tile("w2_raw", [P, 2 * K], U8)
        s2_raw = tile("s2_raw", [P, K], U8)
        gain_sb = tile("gain_sb", [P, PACK], F32)
        prec_sb = tile("prec_sb", [P, PASSES, PACK], F32)
        xg = [tile("xg%d" % a, [P, PACK, S], F32) for a in range(PASSES)]
        xb0 = tile("xb0", [P, S * PACK], BF16)
        xb1 = [
            tile("xb1_front", [P, QUARTER * PACK], BF16, "w1raw0"),
            tile("xb1_second", [P, QUARTER * PACK], BF16),
            tile("xb1_third", [P, QUARTER * PACK], BF16, "w1raw1"),
        ]
        x0_codes = tile("xc0", [P, S], U32, "x10")
        x_plane = [tile("xs%d" % a, [P, S], U8) for a in range(PASSES)]
        w1b = [tile("w1b0", [P, H * PACK], BF16), tile("w1b1", [P, H * PACK], BF16)]
        x1_codes = [
            tile("xc10", [P, QUARTER], U32),
            tile("xc11", [P, QUARTER], U32),
            tile("xc12", [P, QUARTER], U32),
            tile("xc13", [P, QUARTER], U32),
        ]
        w1_codes = [tile("w1c%d" % a, [P, H], U32) for a in range(PASSES)]
        w1_plane = [tile("w1s%d" % a, [P, H], U8) for a in range(PASSES)]
        w2_codes = tile("w2_codes", [P, 2 * K], U8, "x01")
        w2_plane = laid.tile([P, K], U8, name="w2_plane", offset=2 * K, align_bytes=64)
        th = [tile("th%d" % k, [P, n * PACK], F32) for k, (c0, n) in enumerate(chunks)]
        xb1.append(laid.tile([P, QUARTER * PACK], BF16, name="xb1_last", offset=0, align_bytes=64))
        hb = tile("hb", [P, HALF * PACK], BF16)
        h_codes = tile("hc", [P, S], U32)
        h_plane = tile("hs", [P, S], U8)

        def load_x(a, i):
            nc.sync.dma_start(x_sb[a][i][:], x_planes[a, i])

        def load_w1(k):
            r0 = k % 2 * (H // 2)
            nc.sync.dma_start(w1_raw[k][:], w1_rows[k // 2][:, :, r0 : r0 + H // 2])

        nc.vector.memset(s2_raw[:].bitcast(U32), 0)
        nc.vector.memset(wgt_rows[P // 2 : P, :], 0.0)
        make_identity(nc, identity[:])
        nc.sync.dma_start(wgt_rows[0 : P // 2, :], wgt.rearrange("(g r) (c e) -> r g c e", r=GROUP, e=P)[0])
        load_x(0, 0)
        nc.sync.dma_start(offsets[:], offs)
        for i in range(1, PACK):
            load_x(0, i)
        nc.sync.dma_start(w2_raw[:].bitcast(I32), w2_words[0].bitcast(I32))
        load_x(1, 0)
        load_x(1, 1)
        load_w1(0)
        load_x(1, 2)
        load_w1(1)
        load_x(1, 3)
        load_w1(2)
        load_w1(3)
        nc.sync.dma_start(gain_sb[:], gain.rearrange("(p t) -> p t", t=PACK))
        nc.sync.dma_start(prec_sb[:], prec.rearrange("(a p i) -> p a i", a=PASSES, i=PACK))
        scale_rows = w2_scales[0].bitcast(I32).rearrange("(q r) c -> r q c", r=4)
        for r in range(4):
            nc.scalar.dma_start(s2_raw[r:P:32, :].bitcast(I32), scale_rows[r])

        spreads = [(0, 1, nc.vector.tensor_copy), (1, 1, nc.vector.tensor_copy), (2, 2, nc.scalar.copy), (4, 2, nc.scalar.copy), (6, 2, nc.scalar.copy)]
        for h in range(2):
            turned = psum.tile([P, P], F32, name="turned", tag="bank%d" % h)
            nc.tensor.transpose(turned[:], wgt_rows[:], identity[:])
            for c0, n, copy in spreads[2 * h : 3 * h + 2]:
                copy(
                    wgt_spread[:, c0 * P : (c0 + n) * P].rearrange("p (c g r) -> p c g r", g=CAMERAS, r=GROUP),
                    turned[:, 0 : P // 2].rearrange("p (g c) -> p c g", g=CAMERAS)[:, c0 : c0 + n, :].unsqueeze(3).to_broadcast([P, n, CAMERAS, GROUP]),
                )
        for part, (c0, n, copy) in enumerate(spreads):
            back = psum.tile([P, n * P], F32, name="back", tag="bank%d" % (2 + part))
            for c in range(n):
                nc.tensor.transpose(back[:, c * P : (c + 1) * P], wgt_spread[:, (c0 + c) * P : (c0 + c + 1) * P], identity[:])
            copy(wgt_sb[:, c0 * P : (c0 + n) * P], back[:])

        banks = [psum.tile([P, PACK, N1], F32, name="hbank%d" % b, tag="bank%d" % b) for b in range(S // N1)]

        def deal_w2_words():
            nc.scalar.copy(
                w2_codes[:].bitcast(U16).rearrange("p (a i q) -> p a i q", a=PASSES, i=PACK),
                w2_raw[:].bitcast(U16).rearrange("p (a q i) -> p a i q", a=PASSES, i=PACK),
            )

        def deal_w2_scales():
            nc.vector.tensor_copy(
                w2_plane[:].rearrange("p (a i q) -> p a i q", a=PASSES, i=PACK),
                s2_raw[:].rearrange("p (a q i) -> p a i q", a=PASSES, i=PACK),
            )

        def gather(a, i, c0, n):
            window = x_sb[a][i][:].indirect(offsets[:, c0 // 16 : (c0 + n) // 16])
            nc.vector.tensor_tensor(xg[a][:, i, c0 : c0 + n], window, wgt_sb[:, c0 : c0 + n], ALU.mult)

        def rounded_x(a, c0, n):
            if a == 0:
                return xb0[:, c0 * PACK : (c0 + n) * PACK]
            return xb1[c0 // QUARTER][:, c0 % QUARTER * PACK : (c0 % QUARTER + n) * PACK]

        def weave_pair(a, i0, c0, n):
            nc.scalar.copy(
                rounded_x(a, c0, n).rearrange("p (c i) -> p c i", i=PACK)[:, :, i0 : i0 + 2],
                xg[a][:, i0 : i0 + 2, c0 : c0 + n].rearrange("p i c -> p c i"),
            )

        def weave_four(a, c0, n, copy=nc.scalar.copy):
            copy(
                rounded_x(a, c0, n).rearrange("p (c e i) -> p c i e", e=PACK, i=PACK),
                xg[a][:, :, c0 : c0 + n].rearrange("p i (c e) -> p c i e", e=PACK),
            )

        def codes_x(a, c0, n):
            if a == 0:
                return x0_codes[:, c0 : c0 + n].bitcast(E4M3X4)
            return x1_codes[c0 // QUARTER][:, c0 % QUARTER : c0 % QUARTER + n].bitcast(E4M3X4)

        def quant_x(a, c0, n):
            nc.vector.quantize_mx(codes_x(a, c0, n), x_plane[a][:, c0 : c0 + n], rounded_x(a, c0, n))

        def cast_w1(k, copy):
            m0 = k % 2 * (P // 2)
            copy(
                w1b[k // 2][:].rearrange("p (t m i) -> p m i t", t=PACK, i=PACK)[:, m0 : m0 + P // 2, :, :],
                w1_raw[k][:].rearrange("p i (m t) -> p m i t", t=PACK),
            )

        def quant_w1(a, c0=0, n=H):
            nc.vector.quantize_mx(w1_codes[a][:, c0 : c0 + n].bitcast(E4M3X4), w1_plane[a][:, c0 : c0 + n], w1b[a][:, c0 * PACK : (c0 + n) * PACK])

        def encode_pass(b, a):
            for t in range(PACK):
                nc.tensor.matmul_mx(
                    banks[b][:, t, :],
                    lhsT=w1_codes[a][:, t * P : (t + 1) * P].bitcast(E4M3X4),
                    lhsT_scale=w1_plane[a][:, t * P : (t + 1) * P],
                    rhs=codes_x(a, b * N1, N1),
                    rhs_scale=x_plane[a][:, b * N1 : (b + 1) * N1],
                    start=(a == 0 and t == 0),
                    stop=(a == PASSES - 1 and t == PACK - 1),
                )

        def close_quarter(q):
            quant_x(1, q * QUARTER, QUARTER)
            encode_pass(2 * q, 1)
            encode_pass(2 * q + 1, 1)

        def tanh(b, c0=0, n=N1):
            k = b if b < 2 else b // 2 + 1
            first = b * BANK - chunks[k][0] * PACK
            nc.scalar.activation(
                th[k][:, first : first + BANK].rearrange("p (n t) -> p n t", t=PACK)[:, c0 : c0 + n, :],
                banks[b][:].rearrange("p t n -> p n t")[:, c0 : c0 + n, :],
                ACT.Tanh,
            )

        def rounded_h(k):
            first = min(chunks[k][0], QUARTER) * PACK
            return hb[:, first : first + chunks[k][1] * PACK]

        def apply_gain(k, engine, first=0, n=None):
            n = n or chunks[k][1]
            engine.tensor_tensor(
                rounded_h(k).rearrange("p (n t) -> p n t", t=PACK)[:, first : first + n, :],
                th[k][:].rearrange("p (n t) -> p n t", t=PACK)[:, first : first + n, :],
                gain_sb[:].unsqueeze(1).to_broadcast([P, n, PACK]),
                ALU.mult,
            )

        def quant_h(k):
            c0, n = chunks[k]
            nc.vector.quantize_mx(h_codes[:, c0 : c0 + n].bitcast(E4M3X4), h_plane[:, c0 : c0 + n], rounded_h(k))

        decoded = []

        def subtract(k, a, i0, count):
            c0, n = chunks[k]
            cols = slice(c0, c0 + n)
            bank = psum.tile([P, count, n], F32, name="rbank", tag="bank%d" % (len(decoded) % RING))
            decoded.append(bank)
            for u in range(count):
                g = a * PACK + i0 + u
                nc.tensor.matmul_mx(
                    bank[:, u, :],
                    lhsT=w2_codes[:, g * 2 * P : (g + 1) * 2 * P].bitcast(E2M1X4),
                    lhsT_scale=w2_plane[:, g * P : (g + 1) * P],
                    rhs=h_codes[:, cols].bitcast(E4M3X4),
                    rhs_scale=h_plane[:, cols],
                    start=True,
                    stop=True,
                )
            rows = xg[a][:, i0 : i0 + count, cols]
            nc.vector.tensor_tensor(rows, bank[:], rows, ALU.subtract)

        def square(c0, n, a, i0, count):
            for i in range(i0, i0 + count):
                nc.scalar.activation(xg[a][:, i, c0 : c0 + n], xg[a][:, i, c0 : c0 + n], ACT.Square, scale=prec_sb[:, a, i : i + 1])

        def store(c0, n, a, i0, count, queue=nc.sync):
            queue.dma_start(out_rows[a][:, i0 : i0 + count, c0 : c0 + n], xg[a][:, i0 : i0 + count, c0 : c0 + n])

        def finish(c0, n, a, i0, count, queue=nc.sync):
            square(c0, n, a, i0, count)
            store(c0, n, a, i0, count, queue)

        for c0, n in ((0, N1), (N1, N1), (QUARTER, QUARTER), (HALF, QUARTER), (3 * QUARTER, QUARTER)):
            gather(0, 0, c0, n)
        gather(0, 1, 0, S)
        weave_pair(0, 0, 0, S)
        deal_w2_words()
        gather(0, 2, 0, S)
        gather(0, 3, 0, S)
        weave_pair(0, 2, 0, S)
        gather(1, 0, 0, S)
        gather(1, 1, 0, S)
        quant_x(0, 0, S)
        cast_w1(0, nc.scalar.copy)
        weave_pair(1, 0, 0, QUARTER)
        weave_pair(1, 0, QUARTER, QUARTER)
        gather(1, 2, 0, S)
        cast_w1(1, nc.scalar.copy)
        weave_pair(1, 0, HALF, QUARTER)
        quant_w1(0)
        for b in range(S // N1):
            encode_pass(b, 0)
        for c0, n in ((0, N1), (N1, N1), (QUARTER, 3 * QUARTER)):
            gather(1, 3, c0, n)
        weave_pair(1, 2, 0, N1)
        weave_pair(1, 2, N1, N1)
        cast_w1(2, nc.scalar.copy)
        quant_x(1, 0, QUARTER)
        cast_w1(3, nc.vector.tensor_copy)
        weave_four(1, 7 * N1, N1, nc.vector.tensor_copy)
        quant_w1(1, 0, H // 2)
        quant_w1(1, H // 2, H // 2)
        encode_pass(0, 1)
        encode_pass(1, 1)
        weave_pair(1, 2, QUARTER, QUARTER)
        weave_pair(1, 2, HALF, QUARTER)
        weave_four(1, 6 * N1, N1)
        deal_w2_scales()
        close_quarter(1)
        close_quarter(2)
        close_quarter(3)
        tanh(0, 0, N1 // 2)
        tanh(0, N1 // 2, N1 // 2)
        for b in range(1, 8):
            tanh(b)
        apply_gain(0, nc.vector, 0, N1 // 2)
        apply_gain(0, nc.vector, N1 // 2, N1 // 2)
        apply_gain(1, nc.vector)
        quant_h(0)
        apply_gain(2, nc.vector, 0, N1)
        quant_h(1)
        apply_gain(2, nc.vector, N1, N1)
        subtract(0, 0, 0, 4)
        finish(*chunks[0], 0, 0, 4)
        quant_h(2)
        apply_gain(3, nc.gpsimd)
        subtract(1, 0, 0, 4)
        finish(*chunks[1], 0, 0, 4)
        subtract(0, 1, 0, 4)
        finish(*chunks[0], 1, 0, 4)
        subtract(1, 1, 0, 4)
        finish(*chunks[1], 1, 0, 4)
        subtract(2, 0, 0, 2)
        finish(*chunks[2], 0, 0, 2)
        subtract(2, 0, 2, 2)
        finish(*chunks[2], 0, 2, 2)
        quant_h(3)
        apply_gain(4, nc.gpsimd)
        subtract(2, 1, 0, 2)
        finish(*chunks[2], 1, 0, 2)
        subtract(2, 1, 2, 2)
        finish(*chunks[2], 1, 2, 2)
        subtract(3, 0, 0, 2)
        finish(*chunks[3], 0, 0, 2)
        subtract(3, 0, 2, 2)
        finish(*chunks[3], 0, 2, 2)
        subtract(3, 1, 0, 2)
        finish(*chunks[3], 1, 0, 2)
        quant_h(4)
        subtract(3, 1, 2, 2)
        finish(*chunks[3], 1, 2, 2)
        subtract(4, 0, 0, 2)
        finish(*chunks[4], 0, 0, 2)
        subtract(4, 0, 2, 2)
        finish(*chunks[4], 0, 2, 2)
        subtract(4, 1, 0, 2)
        finish(*chunks[4], 1, 0, 2)
        subtract(4, 1, 2, 1)
        finish(*chunks[4], 1, 2, 1)
        subtract(4, 1, 3, 1)
        finish(*chunks[4], 1, 3, 1, nc.scalar)
